import numpy as np
import ml_dtypes


def mxq(x, axis, fmt="e4m3"):
    dtype, down = {"e4m3": (ml_dtypes.float8_e4m3fn, 7), "e5m2": (ml_dtypes.float8_e5m2, 14)}[fmt]
    v = np.moveaxis(np.asarray(x, np.float32).astype(ml_dtypes.bfloat16).astype(np.float64), axis, -1)
    blocks = v.reshape(v.shape[:-1] + (-1, 32))
    amax = np.abs(blocks).max(-1, keepdims=True)
    byte = np.maximum(np.where(amax > 0, np.frexp(amax)[1] - 1 + 127, 0) - down, 1)
    scale = np.exp2(byte - 127.0)
    codes = (blocks / scale).astype(np.float32).astype(dtype).astype(np.float64)
    return np.moveaxis((codes * scale).reshape(v.shape), -1, axis)


WIDE = False


def mx_kscale(k):
    if not WIDE:
        return np.ones(k)
    levels = np.array([10, -10, 5, -5, 0])
    if k % 512:
        return np.exp2(np.random.permutation(np.resize(levels, k // 32))).repeat(32)
    a = np.empty((k // 512, 16))
    for p in range(k // 512):
        a[p, :8] = np.random.permutation(np.resize(levels, 8))
        for g in range(8):
            far = levels[np.abs(levels - a[p, g]) >= 10]
            a[p, g + 8] = far[np.random.randint(len(far))]
    return np.exp2(a.ravel()).repeat(32)


def f64(x):
    return np.asarray(x).astype(np.float64)


def striped8(idx):
    return np.concatenate([v.reshape(-1, 16).T for v in idx]).astype(np.uint16)


def unstriped8(offs):
    return np.stack([offs[16 * g:16 * g + 16].T.reshape(-1) for g in range(8)]).astype(np.int64)


G, K, M, T, S = 2, 1024, 256, 2048, 512


def setup_inputs():
    n = np.random.standard_normal
    s = mx_kscale(K)[:, None]
    return {
        "xT": (n((K, T)) * s).astype(np.float32),
        "w": (n((K, M)) / np.sqrt(K) / s).astype(np.float32),
        "wgt": np.repeat(np.random.uniform(0.5, 2.0, (8, G * S)), 16, axis=0).astype(np.float32),
        "offs": striped8(np.stack([np.concatenate([np.random.permutation(T)[:S] for _ in range(G)]) for _ in range(8)])),
    }


def reference(xT, w, wgt, offs):
    idx = unstriped8(offs)
    group = np.arange(K) % 512 // 64
    xg = f64(wgt)[np.arange(K) // 4 % 128] * f64(xT)[np.arange(K)[:, None], idx[group]]
    xT_ = mxq(xg, 0, "e4m3")
    xT_ = xT_.reshape(K, G, S).sum(1)
    w_ = mxq(f64(w), 0, "e4m3")
    y = w_.T @ xT_
    return y

@@ -1,0 +1,153 @@
+from contextlib import ExitStack
+
+import concourse.mybir as mybir
+
+G, K, M, T, S = 2, 1024, 256, 2048, 512
+FLOPS = 2 * G * K * M * S
+
+F32 = mybir.dt.float32
+BF16 = mybir.dt.bfloat16
+U32 = mybir.dt.uint32
+U16 = mybir.dt.uint16
+U8 = mybir.dt.uint8
+FP8X4 = mybir.dt.float8_e4m3fn_x4
+MULT = mybir.AluOpType.mult
+
+P = 128
+PACK = 4
+K_PASS = P * PACK
+LIST = 16
+CHUNKS = [(0, 256), (256, 128), (384, 128)]
+
+
+def tile_list_hbag_none_kernel(tc, xT, w, wgt, offs, out):
+    nc = tc.nc
+    with ExitStack() as ctx:
+        keep = ctx.enter_context(tc.tile_pool(name="keep", bufs=1))
+        psum = ctx.enter_context(tc.psum_pool(name="psum", bufs=1))
+
+        offsets = keep.tile([P, G * S // LIST], U16, name="offsets")
+        weights = [keep.tile([P, S], F32, name=f"weights{c}") for c in range(G)]
+        plane = [[keep.tile([P, T], F32, name=f"plane{a}_{i}") for i in range(PACK)] for a in range(2)]
+        picked = [keep.tile([P, PACK, G * S], F32, name=f"picked{a}") for a in range(2)]
+        w_raw = [keep.tile([P, PACK, M], F32, name=f"w_raw{a}") for a in range(2)]
+        w_bf = [keep.tile([P, M, PACK], BF16, name=f"w_bf{a}", align_bytes=64) for a in range(2)]
+        w_codes = [keep.tile([P, M], U32, name=f"w_codes{a}", align_bytes=64) for a in range(2)]
+        w_scales = [keep.tile([P, M], U8, name=f"w_scales{a}", align_bytes=64) for a in range(2)]
+        x_bf = [keep.tile([P, G * S, PACK], BF16, name=f"x_bf{a}", align_bytes=64) for a in range(2)]
+        x_codes = [keep.tile([P, G * S], U32, name=f"x_codes{a}", align_bytes=64) for a in range(2)]
+        x_scales = [keep.tile([P, G * S], U8, name=f"x_scales{a}", align_bytes=64) for a in range(2)]
+        acc = [[psum.tile([P, n], F32, name=f"acc{j0}_{m}") for m in range(2)] for j0, n in CHUNKS]
+        staged = [keep.tile([P, 2, n], F32, name=f"staged{j0}") for j0, n in CHUNKS]
+
+        x_rows = xT.rearrange("(a p i) t -> a i p t", a=2, i=PACK)
+        w_rows = w.rearrange("(a p i) n -> a p i n", a=2, i=PACK)
+        out_rows = out.rearrange("(m p) j -> p m j", p=P)
+
+        def load_plane(a, i):
+            nc.sync.dma_start(out=plane[a][i][:], in_=x_rows[a, i])
+
+        def gather(a, i, c, j0, n):
+            e0 = c * S + j0
+            nc.vector.tensor_tensor(
+                picked[a][:, i, e0 : e0 + n],
+                plane[a][i][:].indirect(offsets[:, e0 // LIST : (e0 + n) // LIST]),
+                weights[c][:, j0 : j0 + n],
+                MULT,
+            )
+
+        def interleave(copy, dst, src):
+            copy(dst.rearrange("p (c e) t -> p c t e", e=4), src.rearrange("p t (c e) -> p c t e", e=4))
+
+        def x_interleave(copy, a, c, j0, n):
+            e0 = c * S + j0
+            interleave(copy, x_bf[a][:, e0 : e0 + n, :], picked[a][:, :, e0 : e0 + n])
+
+        def x_quantize(a, c, j0, n):
+            e0 = c * S + j0
+            nc.vector.quantize_mx(
+                out=x_codes[a][:, e0 : e0 + n].bitcast(FP8X4),
+                scales=x_scales[a][:, e0 : e0 + n],
+                in_=x_bf[a][:, e0 : e0 + n, :].rearrange("p j t -> p (j t)"),
+            )
+
+        def w_quantize(a):
+            nc.vector.quantize_mx(
+                out=w_codes[a][:].bitcast(FP8X4),
+                scales=w_scales[a][:],
+                in_=w_bf[a][:].rearrange("p n t -> p (n t)"),
+            )
+
+        def multiply(a, c, q):
+            j0, n = CHUNKS[q]
+            e0 = c * S + j0
+            for m in range(2):
+                nc.tensor.matmul_mx(
+                    out=acc[q][m][:],
+                    lhsT=w_codes[a][:, m * P : (m + 1) * P].bitcast(FP8X4),
+                    lhsT_scale=w_scales[a][:, m * P : (m + 1) * P],
+                    rhs=x_codes[a][:, e0 : e0 + n].bitcast(FP8X4),
+                    rhs_scale=x_scales[a][:, e0 : e0 + n],
+                    start=(a == 0 and c == 0),
+                    stop=(a == 1 and c == G - 1),
+                )
+
+        def store(q, copies):
+            j0, n = CHUNKS[q]
+            for m in range(2):
+                copies[m](staged[q][:, m, :], acc[q][m][:])
+            nc.sync.dma_start(out=out_rows[:, :, j0 : j0 + n], in_=staged[q][:])
+
+        act, dve = nc.scalar.copy, nc.vector.tensor_copy
+
+        nc.sync.dma_start(offsets[:], offs)
+        nc.sync.dma_start(out=weights[0][:], in_=wgt[:, 0:S])
+        load_plane(0, 0)
+        nc.sync.dma_start(out=weights[1][:], in_=wgt[:, S : 2 * S])
+        for i in range(1, PACK):
+            load_plane(0, i)
+        load_plane(1, 0)
+        load_plane(1, 1)
+        nc.sync.dma_start(out=w_raw[0][:], in_=w_rows[0])
+        load_plane(1, 2)
+        load_plane(1, 3)
+        nc.sync.dma_start(out=w_raw[1][:], in_=w_rows[1])
+
+        for i in range(PACK):
+            for c in range(G):
+                gather(0, i, c, 0, S)
+        for c in range(G):
+            x_interleave(act, 0, c, 0, S)
+        interleave(act, w_bf[0][:], w_raw[0][:])
+        for i in range(2):
+            for c in range(G):
+                gather(1, i, c, 0, S)
+        x_quantize(0, 0, 0, S)
+        for c in range(G):
+            gather(1, 2, c, 0, S)
+        w_quantize(0)
+        for q in range(len(CHUNKS)):
+            multiply(0, 0, q)
+
+        for j0, n in CHUNKS:
+            for c in range(G):
+                gather(1, 3, c, j0, n)
+        for j0, n in CHUNKS:
+            for c in range(G):
+                x_interleave(act, 1, c, j0, n)
+        x_quantize(0, 1, 0, S)
+        for q in range(len(CHUNKS)):
+            multiply(0, 1, q)
+        interleave(dve, w_bf[1][:], w_raw[1][:])
+        x_quantize(1, 0, *CHUNKS[0])
+        w_quantize(1)
+        x_quantize(1, 1, *CHUNKS[0])
+        multiply(1, 0, 0)
+        multiply(1, 1, 0)
+        for q in (1, 2):
+            for c in range(G):
+                x_quantize(1, c, *CHUNKS[q])
+                multiply(1, c, q)
+        store(0, (act, act))
+        store(1, (dve, dve))
+        store(2, (dve, act))

@@ -15,7 +15,6 @@ MULT = mybir.AluOpType.mult
 
 P = 128
 PACK = 4
-K_PASS = P * PACK
 LIST = 16
 CHUNKS = [(0, 256), (256, 128), (384, 128)]
 
@@ -27,12 +26,12 @@ def tile_list_hbag_none_kernel(tc, xT, w, wgt, offs, out):
         psum = ctx.enter_context(tc.psum_pool(name="psum", bufs=1))
 
         offsets = keep.tile([P, G * S // LIST], U16, name="offsets")
-        weights = [keep.tile([P, S], F32, name=f"weights{c}") for c in range(G)]
-        plane = [[keep.tile([P, T], F32, name=f"plane{a}_{i}") for i in range(PACK)] for a in range(2)]
-        picked = [keep.tile([P, PACK, G * S], F32, name=f"picked{a}") for a in range(2)]
+        weights = [keep.tile([P, S], F32, name=f"weights{c}", align_bytes=64) for c in range(G)]
+        plane = [[keep.tile([P, T], F32, name=f"plane{a}_{i}", tag=f"plane{a}_{i}", align_bytes=64) for i in range(PACK)] for a in range(2)]
+        picked = [keep.tile([P, PACK, G, S], F32, name=f"picked{a}") for a in range(2)]
         w_raw = [keep.tile([P, PACK, M], F32, name=f"w_raw{a}") for a in range(2)]
         w_bf = [keep.tile([P, M, PACK], BF16, name=f"w_bf{a}", align_bytes=64) for a in range(2)]
-        w_codes = [keep.tile([P, M], U32, name=f"w_codes{a}", align_bytes=64) for a in range(2)]
+        w_codes = {}
         w_scales = [keep.tile([P, M], U8, name=f"w_scales{a}", align_bytes=64) for a in range(2)]
         x_bf = [keep.tile([P, G * S, PACK], BF16, name=f"x_bf{a}", align_bytes=64) for a in range(2)]
         x_codes = [keep.tile([P, G * S], U32, name=f"x_codes{a}", align_bytes=64) for a in range(2)]
@@ -47,47 +46,63 @@ def tile_list_hbag_none_kernel(tc, xT, w, wgt, offs, out):
         def load_plane(a, i):
             nc.sync.dma_start(out=plane[a][i][:], in_=x_rows[a, i])
 
+        def load_w(a):
+            nc.sync.dma_start(out=w_raw[a][:], in_=w_rows[a])
+
         def gather(a, i, c, j0, n):
             e0 = c * S + j0
             nc.vector.tensor_tensor(
-                picked[a][:, i, e0 : e0 + n],
+                picked[a][:, i, c, j0 : j0 + n],
                 plane[a][i][:].indirect(offsets[:, e0 // LIST : (e0 + n) // LIST]),
                 weights[c][:, j0 : j0 + n],
                 MULT,
             )
 
-        def interleave(copy, dst, src):
-            copy(dst.rearrange("p (c e) t -> p c t e", e=4), src.rearrange("p t (c e) -> p c t e", e=4))
+        def column(a, c, q):
+            j0, n = CHUNKS[q]
+            return c * S + j0
 
-        def x_interleave(copy, a, c, j0, n):
-            e0 = c * S + j0
-            interleave(copy, x_bf[a][:, e0 : e0 + n, :], picked[a][:, :, e0 : e0 + n])
-
-        def x_quantize(a, c, j0, n):
-            e0 = c * S + j0
-            nc.vector.quantize_mx(
-                out=x_codes[a][:, e0 : e0 + n].bitcast(FP8X4),
-                scales=x_scales[a][:, e0 : e0 + n],
-                in_=x_bf[a][:, e0 : e0 + n, :].rearrange("p j t -> p (j t)"),
+        def w_interleave(copy, a):
+            copy(
+                w_bf[a][:].rearrange("p (u e) t -> p u t e", e=4),
+                w_raw[a][:].rearrange("p t (u e) -> p u t e", e=4),
             )
 
-        def w_quantize(a):
+        def x_interleave(copy, a, col, picks, j0, n, lanes=slice(0, PACK)):
+            count = picks.stop - picks.start
+            copy(
+                x_bf[a][:, col : col + count * n, lanes].rearrange("p (c u e) t -> p c u t e", c=count, e=4),
+                picked[a][:, lanes, picks, j0 : j0 + n].rearrange("p t c (u e) -> p c u t e", e=4),
+            )
+
+        def x_pairs(copy, col, c, j0, n, lanes):
+            copy(x_bf[1][:, col : col + n, lanes], picked[1][:, lanes, c, j0 : j0 + n].rearrange("p t j -> p j t"))
+
+        def x_quantize(a, col, n):
+            nc.vector.quantize_mx(
+                out=x_codes[a][:, col : col + n].bitcast(FP8X4),
+                scales=x_scales[a][:, col : col + n],
+                in_=x_bf[a][:, col : col + n, :].rearrange("p j t -> p (j t)"),
+            )
+
+        def w_quantize(a, after):
+            w_codes[a] = keep.tile([P, M], U32, name=f"w_codes{a}", tag=after, align_bytes=64)
             nc.vector.quantize_mx(
                 out=w_codes[a][:].bitcast(FP8X4),
                 scales=w_scales[a][:],
                 in_=w_bf[a][:].rearrange("p n t -> p (n t)"),
             )
 
-        def multiply(a, c, q):
-            j0, n = CHUNKS[q]
-            e0 = c * S + j0
-            for m in range(2):
+        def multiply(a, c, q, ms=(0, 1)):
+            n = CHUNKS[q][1]
+            col = column(a, c, q)
+            for m in ms:
                 nc.tensor.matmul_mx(
                     out=acc[q][m][:],
                     lhsT=w_codes[a][:, m * P : (m + 1) * P].bitcast(FP8X4),
                     lhsT_scale=w_scales[a][:, m * P : (m + 1) * P],
-                    rhs=x_codes[a][:, e0 : e0 + n].bitcast(FP8X4),
-                    rhs_scale=x_scales[a][:, e0 : e0 + n],
+                    rhs=x_codes[a][:, col : col + n].bitcast(FP8X4),
+                    rhs_scale=x_scales[a][:, col : col + n],
                     start=(a == 0 and c == 0),
                     stop=(a == 1 and c == G - 1),
                 )
@@ -107,46 +122,42 @@ def tile_list_hbag_none_kernel(tc, xT, w, wgt, offs, out):
         for i in range(1, PACK):
             load_plane(0, i)
         load_plane(1, 0)
+        load_w(0)
         load_plane(1, 1)
-        nc.sync.dma_start(out=w_raw[0][:], in_=w_rows[0])
         load_plane(1, 2)
+        load_w(1)
         load_plane(1, 3)
-        nc.sync.dma_start(out=w_raw[1][:], in_=w_rows[1])
 
         for i in range(PACK):
             for c in range(G):
                 gather(0, i, c, 0, S)
         for c in range(G):
-            x_interleave(act, 0, c, 0, S)
-        interleave(act, w_bf[0][:], w_raw[0][:])
-        for i in range(2):
-            for c in range(G):
-                gather(1, i, c, 0, S)
-        x_quantize(0, 0, 0, S)
+            x_interleave(act, 0, c * S, slice(c, c + 1), 0, S)
+        w_interleave(act, 0)
+        for c in range(G):
+            gather(1, 0, c, 0, S)
+        x_quantize(0, 0, S)
+        for c in range(G):
+            gather(1, 1, c, 0, S)
+        x_quantize(0, S, S)
+        for c in range(G):
+            x_pairs(act, c * S, c, 0, S, slice(0, 2))
         for c in range(G):
             gather(1, 2, c, 0, S)
-        w_quantize(0)
-        for q in range(len(CHUNKS)):
-            multiply(0, 0, q)
+        w_quantize(0, "plane1_2")
+        for c in range(G):
+            for q in range(len(CHUNKS)):
+                multiply(0, c, q)
+        w_interleave(act, 1)
 
-        for j0, n in CHUNKS:
-            for c in range(G):
-                gather(1, 3, c, j0, n)
-        for j0, n in CHUNKS:
-            for c in range(G):
-                x_interleave(act, 1, c, j0, n)
-        x_quantize(0, 1, 0, S)
         for q in range(len(CHUNKS)):
-            multiply(0, 1, q)
-        interleave(dve, w_bf[1][:], w_raw[1][:])
-        x_quantize(1, 0, *CHUNKS[0])
-        w_quantize(1)
-        x_quantize(1, 1, *CHUNKS[0])
-        multiply(1, 0, 0)
-        multiply(1, 1, 0)
-        for q in (1, 2):
             for c in range(G):
-                x_quantize(1, c, *CHUNKS[q])
+                gather(1, 3, c, *CHUNKS[q])
+                x_pairs(act, column(1, c, q), c, *CHUNKS[q], slice(2, 4))
+        w_quantize(1, "plane1_3")
+        for q in range(len(CHUNKS)):
+            for c in range(G):
+                x_quantize(1, column(1, c, q), CHUNKS[q][1])
                 multiply(1, c, q)
         store(0, (act, act))
         store(1, (dve, dve))

@@ -39,6 +39,9 @@ def tile_list_hbag_none_kernel(tc, xT, w, wgt, offs, out):
         acc = [[psum.tile([P, n], F32, name=f"acc{j0}_{m}") for m in range(2)] for j0, n in CHUNKS]
         staged = [keep.tile([P, 2, n], F32, name=f"staged{j0}") for j0, n in CHUNKS]
 
+        w_rows32 = keep.tile([P, 2, 32], F32, name="wgt_rows", align_bytes=64)
+        w_cols32 = keep.tile([P, 2, 32], F32, name="wgt_cols", align_bytes=64)
+        w_spread = [keep.tile([P, 16, 2, 16], F32, name=f"wgt_spread{c}", align_bytes=64) for c in range(G)]
         x_rows = xT.rearrange("(a p i) t -> a i p t", a=2, i=PACK)
         w_rows = w.rearrange("(a p i) n -> a p i n", a=2, i=PACK)
         out_rows = out.rearrange("(m p) j -> p m j", p=P)
@@ -115,10 +118,12 @@ def tile_list_hbag_none_kernel(tc, xT, w, wgt, offs, out):
 
         act, dve = nc.scalar.copy, nc.vector.tensor_copy
 
-        nc.sync.dma_start(offsets[:], offs)
-        nc.sync.dma_start(out=weights[0][:], in_=wgt[:, 0:S])
+        wgt_rows = wgt.rearrange("(q h r) (b s) -> q r b h s", q=4, h=2, s=32)
+        for q in range(4):
+            queue = nc.sync if q % 2 == 0 else nc.scalar
+            queue.dma_start(out=w_rows32[32 * q : 32 * (q + 1), :, :], in_=wgt_rows[q, 0])
         load_plane(0, 0)
-        nc.sync.dma_start(out=weights[1][:], in_=wgt[:, S : 2 * S])
+        nc.sync.dma_start(offsets[:], offs)
         for i in range(1, PACK):
             load_plane(0, i)
         load_plane(1, 0)
@@ -127,6 +132,16 @@ def tile_list_hbag_none_kernel(tc, xT, w, wgt, offs, out):
         load_plane(1, 2)
         load_w(1)
         load_plane(1, 3)
+
+        for h in range(2):
+            nc.vector.transpose(w_cols32[:, h, :], w_rows32[:, h, :])
+        for c, copy in enumerate((dve, dve)):
+            copy(
+                w_spread[c][:],
+                w_cols32[:, :, 16 * c : 16 * (c + 1)].rearrange("p h b -> p b h").unsqueeze(3).to_broadcast([P, 16, 2, 16]),
+            )
+        for c in range(G):
+            nc.vector.transpose(weights[c][:], w_spread[c][:].rearrange("p b h r -> p (b h r)"))
 
         for i in range(PACK):
             for c in range(G):
@@ -150,15 +165,19 @@ def tile_list_hbag_none_kernel(tc, xT, w, wgt, offs, out):
                 multiply(0, c, q)
         w_interleave(act, 1)
 
-        for q in range(len(CHUNKS)):
-            for c in range(G):
-                gather(1, 3, c, *CHUNKS[q])
-                x_pairs(act, column(1, c, q), c, *CHUNKS[q], slice(2, 4))
+        half = S // 2
+        for c, j0, n in [(0, 0, 128), (0, 128, 128), (1, 0, half), (0, half, half), (1, half, half)]:
+            gather(1, 3, c, j0, n)
+        pieces = [(0, 0, half, (0,)), (1, 0, half, (0,)), (0, half, half, (1, 2)), (1, *CHUNKS[1], (1,)), (1, *CHUNKS[2], (2,))]
+        for c, j0, n in [(0, 0, 128), (0, 128, 128)] + [piece[:3] for piece in pieces[1:]]:
+            x_pairs(act, c * S + j0, c, j0, n, slice(2, 4))
         w_quantize(1, "plane1_3")
-        for q in range(len(CHUNKS)):
-            for c in range(G):
-                x_quantize(1, column(1, c, q), CHUNKS[q][1])
+        for c, j0, n, chunks in pieces:
+            x_quantize(1, c * S + j0, n)
+            for q in chunks:
                 multiply(1, c, q)
-        store(0, (act, act))
+        for m in range(2):
+            act(staged[0][:, m, :], acc[0][m][:])
+            nc.sync.dma_start(out=out_rows[:, m, 0:half], in_=staged[0][:, m, :])
         store(1, (dve, dve))
         store(2, (dve, act))

@@ -26,9 +26,9 @@ def tile_list_hbag_none_kernel(tc, xT, w, wgt, offs, out):
         psum = ctx.enter_context(tc.psum_pool(name="psum", bufs=1))
 
         offsets = keep.tile([P, G * S // LIST], U16, name="offsets")
-        weights = [keep.tile([P, S], F32, name=f"weights{c}", align_bytes=64) for c in range(G)]
+        weights = keep.tile([P, G * S], F32, name="weights", align_bytes=64)
         plane = [[keep.tile([P, T], F32, name=f"plane{a}_{i}", tag=f"plane{a}_{i}", align_bytes=64) for i in range(PACK)] for a in range(2)]
-        picked = [keep.tile([P, PACK, G, S], F32, name=f"picked{a}") for a in range(2)]
+        picked = [keep.tile([P, PACK, G * S], F32, name=f"picked{a}") for a in range(2)]
         w_raw = [keep.tile([P, PACK, M], F32, name=f"w_raw{a}") for a in range(2)]
         w_bf = [keep.tile([P, M, PACK], BF16, name=f"w_bf{a}", align_bytes=64) for a in range(2)]
         w_codes = {}
@@ -41,7 +41,7 @@ def tile_list_hbag_none_kernel(tc, xT, w, wgt, offs, out):
 
         w_rows32 = keep.tile([P, 2, 32], F32, name="wgt_rows", align_bytes=64)
         w_cols32 = keep.tile([P, 2, 32], F32, name="wgt_cols", align_bytes=64)
-        w_spread = [keep.tile([P, 16, 2, 16], F32, name=f"wgt_spread{c}", align_bytes=64) for c in range(G)]
+        w_spread = [keep.tile([P, 8, 2, 2, 16], F32, name=f"wgt_spread{c}", align_bytes=64) for c in range(G)]
         x_rows = xT.rearrange("(a p i) t -> a i p t", a=2, i=PACK)
         w_rows = w.rearrange("(a p i) n -> a p i n", a=2, i=PACK)
         out_rows = out.rearrange("(m p) j -> p m j", p=P)
@@ -52,12 +52,11 @@ def tile_list_hbag_none_kernel(tc, xT, w, wgt, offs, out):
         def load_w(a):
             nc.sync.dma_start(out=w_raw[a][:], in_=w_rows[a])
 
-        def gather(a, i, c, j0, n):
-            e0 = c * S + j0
+        def gather(a, i, e0=0, n=G * S):
             nc.vector.tensor_tensor(
-                picked[a][:, i, c, j0 : j0 + n],
+                picked[a][:, i, e0 : e0 + n],
                 plane[a][i][:].indirect(offsets[:, e0 // LIST : (e0 + n) // LIST]),
-                weights[c][:, j0 : j0 + n],
+                weights[:, e0 : e0 + n],
                 MULT,
             )
 
@@ -71,15 +70,14 @@ def tile_list_hbag_none_kernel(tc, xT, w, wgt, offs, out):
                 w_raw[a][:].rearrange("p t (u e) -> p u t e", e=4),
             )
 
-        def x_interleave(copy, a, col, picks, j0, n, lanes=slice(0, PACK)):
-            count = picks.stop - picks.start
-            copy(
-                x_bf[a][:, col : col + count * n, lanes].rearrange("p (c u e) t -> p c u t e", c=count, e=4),
-                picked[a][:, lanes, picks, j0 : j0 + n].rearrange("p t c (u e) -> p c u t e", e=4),
-            )
+        def x_pairs(copy, a, h, e0, n):
+            copy(x_bf[a][:, e0 : e0 + n, 2 * h : 2 * h + 2], picked[a][:, 2 * h : 2 * h + 2, e0 : e0 + n].rearrange("p t j -> p j t"))
 
-        def x_pairs(copy, col, c, j0, n, lanes):
-            copy(x_bf[1][:, col : col + n, lanes], picked[1][:, lanes, c, j0 : j0 + n].rearrange("p t j -> p j t"))
+        def x_interleave(copy, a, e0, n):
+            copy(
+                x_bf[a][:, e0 : e0 + n, :].rearrange("p (u e) t -> p u t e", e=4),
+                picked[a][:, :, e0 : e0 + n].rearrange("p t (u e) -> p u t e", e=4),
+            )
 
         def x_quantize(a, col, n):
             nc.vector.quantize_mx(
@@ -118,10 +116,8 @@ def tile_list_hbag_none_kernel(tc, xT, w, wgt, offs, out):
 
         act, dve = nc.scalar.copy, nc.vector.tensor_copy
 
-        wgt_rows = wgt.rearrange("(q h r) (b s) -> q r b h s", q=4, h=2, s=32)
-        for q in range(4):
-            queue = nc.sync if q % 2 == 0 else nc.scalar
-            queue.dma_start(out=w_rows32[32 * q : 32 * (q + 1), :, :], in_=wgt_rows[q, 0])
+        wgt_rows = wgt.rearrange("(g r) (b s) -> r g b s", r=LIST, s=64)
+        nc.sync.dma_start(out=w_rows32[:].rearrange("p u s -> p (u s)"), in_=wgt_rows[0])
         load_plane(0, 0)
         nc.sync.dma_start(offsets[:], offs)
         for i in range(1, PACK):
@@ -129,8 +125,8 @@ def tile_list_hbag_none_kernel(tc, xT, w, wgt, offs, out):
         load_plane(1, 0)
         load_w(0)
         load_plane(1, 1)
-        load_plane(1, 2)
         load_w(1)
+        load_plane(1, 2)
         load_plane(1, 3)
 
         for h in range(2):
@@ -138,42 +134,44 @@ def tile_list_hbag_none_kernel(tc, xT, w, wgt, offs, out):
         for c, copy in enumerate((dve, dve)):
             copy(
                 w_spread[c][:],
-                w_cols32[:, :, 16 * c : 16 * (c + 1)].rearrange("p h b -> p b h").unsqueeze(3).to_broadcast([P, 16, 2, 16]),
+                w_cols32[:].rearrange("p u (h b) -> p b u h", h=2)[:, 8 * c : 8 * (c + 1)].unsqueeze(4).to_broadcast([P, 8, 2, 2, 16]),
             )
         for c in range(G):
-            nc.vector.transpose(weights[c][:], w_spread[c][:].rearrange("p b h r -> p (b h r)"))
+            nc.vector.transpose(weights[:, c * S : (c + 1) * S], w_spread[c][:].rearrange("p b u h r -> p (b u h r)"))
 
-        for i in range(PACK):
-            for c in range(G):
-                gather(0, i, c, 0, S)
         for c in range(G):
-            x_interleave(act, 0, c * S, slice(c, c + 1), 0, S)
+            gather(0, 0, c * S, S)
+        gather(0, 1)
+        gather(0, 2)
+        for c in range(G):
+            gather(0, 3, c * S, S)
+        for c in range(G):
+            x_interleave(act, 0, c * S, S)
         w_interleave(act, 0)
-        for c in range(G):
-            gather(1, 0, c, 0, S)
+        gather(1, 0)
         x_quantize(0, 0, S)
         for c in range(G):
-            gather(1, 1, c, 0, S)
+            gather(1, 1, c * S, S)
         x_quantize(0, S, S)
+        w_interleave(act, 1)
         for c in range(G):
-            x_pairs(act, c * S, c, 0, S, slice(0, 2))
-        for c in range(G):
-            gather(1, 2, c, 0, S)
+            x_pairs(act, 1, 0, c * S, S)
+        gather(1, 2)
         w_quantize(0, "plane1_2")
         for c in range(G):
             for q in range(len(CHUNKS)):
                 multiply(0, c, q)
-        w_interleave(act, 1)
 
         half = S // 2
         for c, j0, n in [(0, 0, 128), (0, 128, 128), (1, 0, half), (0, half, half), (1, half, half)]:
-            gather(1, 3, c, j0, n)
+            gather(1, 3, c * S + j0, n)
         pieces = [(0, 0, half, (0,)), (1, 0, half, (0,)), (0, half, half, (1, 2)), (1, *CHUNKS[1], (1,)), (1, *CHUNKS[2], (2,))]
         for c, j0, n in [(0, 0, 128), (0, 128, 128)] + [piece[:3] for piece in pieces[1:]]:
-            x_pairs(act, c * S + j0, c, j0, n, slice(2, 4))
-        w_quantize(1, "plane1_3")
-        for c, j0, n, chunks in pieces:
+            x_pairs(act, 1, 1, c * S + j0, n)
+        for number, (c, j0, n, chunks) in enumerate(pieces):
             x_quantize(1, c * S + j0, n)
+            if number == 0:
+                w_quantize(1, "plane1_3")
             for q in chunks:
                 multiply(1, c, q)
         for m in range(2):

@@ -16,6 +16,7 @@ MULT = mybir.AluOpType.mult
 P = 128
 PACK = 4
 LIST = 16
+FIRST = 192
 CHUNKS = [(0, 256), (256, 128), (384, 128)]
 
 
@@ -28,7 +29,8 @@ def tile_list_hbag_none_kernel(tc, xT, w, wgt, offs, out):
         offsets = keep.tile([P, G * S // LIST], U16, name="offsets")
         weights = keep.tile([P, G * S], F32, name="weights", align_bytes=64)
         plane = [[keep.tile([P, T], F32, name=f"plane{a}_{i}", tag=f"plane{a}_{i}", align_bytes=64) for i in range(PACK)] for a in range(2)]
-        picked = [keep.tile([P, PACK, G * S], F32, name=f"picked{a}") for a in range(2)]
+        picked = [keep.tile([P, PACK, G * S], F32, name=f"picked{a}", tag=f"picked{a}", align_bytes=64) for a in range(2)]
+        first = keep.tile([P, 2, FIRST], F32, name="first", tag="first", align_bytes=64)
         w_raw = [keep.tile([P, PACK, M], F32, name=f"w_raw{a}") for a in range(2)]
         w_bf = [keep.tile([P, M, PACK], BF16, name=f"w_bf{a}", align_bytes=64) for a in range(2)]
         w_codes = {}
@@ -52,9 +54,14 @@ def tile_list_hbag_none_kernel(tc, xT, w, wgt, offs, out):
         def load_w(a):
             nc.sync.dma_start(out=w_raw[a][:], in_=w_rows[a])
 
+        def lanes(a, h, e0, n):
+            if (a, h, e0) == (0, 1, 0):
+                return first[:]
+            return picked[a][:, 2 * h : 2 * h + 2, e0 : e0 + n]
+
         def gather(a, i, e0=0, n=G * S):
             nc.vector.tensor_tensor(
-                picked[a][:, i, e0 : e0 + n],
+                lanes(a, i // 2, e0, n)[:, i % 2],
                 plane[a][i][:].indirect(offsets[:, e0 // LIST : (e0 + n) // LIST]),
                 weights[:, e0 : e0 + n],
                 MULT,
@@ -71,7 +78,7 @@ def tile_list_hbag_none_kernel(tc, xT, w, wgt, offs, out):
             )
 
         def x_pairs(copy, a, h, e0, n):
-            copy(x_bf[a][:, e0 : e0 + n, 2 * h : 2 * h + 2], picked[a][:, 2 * h : 2 * h + 2, e0 : e0 + n].rearrange("p t j -> p j t"))
+            copy(x_bf[a][:, e0 : e0 + n, 2 * h : 2 * h + 2], lanes(a, h, e0, n).rearrange("p t j -> p j t"))
 
         def x_interleave(copy, a, e0, n):
             copy(
@@ -104,7 +111,7 @@ def tile_list_hbag_none_kernel(tc, xT, w, wgt, offs, out):
                     lhsT_scale=w_scales[a][:, m * P : (m + 1) * P],
                     rhs=x_codes[a][:, col : col + n].bitcast(FP8X4),
                     rhs_scale=x_scales[a][:, col : col + n],
-                    start=(a == 0 and c == 0),
+                    start=(a == 0 and c == G - 1),
                     stop=(a == 1 and c == G - 1),
                 )
 
@@ -118,15 +125,15 @@ def tile_list_hbag_none_kernel(tc, xT, w, wgt, offs, out):
 
         wgt_rows = wgt.rearrange("(g r) (b s) -> r g b s", r=LIST, s=64)
         nc.sync.dma_start(out=w_rows32[:].rearrange("p u s -> p (u s)"), in_=wgt_rows[0])
-        load_plane(0, 0)
-        nc.sync.dma_start(offsets[:], offs)
-        for i in range(1, PACK):
-            load_plane(0, i)
         load_plane(1, 0)
-        load_w(0)
+        nc.sync.dma_start(offsets[:], offs)
         load_plane(1, 1)
-        load_w(1)
+        for i in range(3):
+            load_plane(0, i)
+        load_w(0)
+        load_plane(0, 3)
         load_plane(1, 2)
+        load_w(1)
         load_plane(1, 3)
 
         for h in range(2):
@@ -140,27 +147,28 @@ def tile_list_hbag_none_kernel(tc, xT, w, wgt, offs, out):
             nc.vector.transpose(weights[:, c * S : (c + 1) * S], w_spread[c][:].rearrange("p b u h r -> p (b u h r)"))
 
         for c in range(G):
-            gather(0, 0, c * S, S)
+            gather(1, 0, c * S, S)
+        gather(1, 1)
+        x_pairs(act, 1, 0, 0, G * S)
+        gather(0, 0)
         gather(0, 1)
-        gather(0, 2)
-        for c in range(G):
-            gather(0, 3, c * S, S)
-        for c in range(G):
-            x_interleave(act, 0, c * S, S)
+        x_pairs(act, 0, 0, 0, S)
+        gather(0, 2, 0, FIRST)
+        gather(0, 2, FIRST, G * S - FIRST)
         w_interleave(act, 0)
-        gather(1, 0)
+        for e0, n in ((0, 192), (192, 320)):
+            gather(0, 3, e0, n)
+            x_pairs(act, 0, 1, e0, n)
+        gather(0, 3, S, S)
+        x_interleave(act, 0, S, S)
+        w_quantize(0, "first")
         x_quantize(0, 0, S)
-        for c in range(G):
-            gather(1, 1, c * S, S)
-        x_quantize(0, S, S)
-        w_interleave(act, 1)
-        for c in range(G):
-            x_pairs(act, 1, 0, c * S, S)
         gather(1, 2)
-        w_quantize(0, "plane1_2")
-        for c in range(G):
-            for q in range(len(CHUNKS)):
+        x_quantize(0, S, S)
+        for q in range(len(CHUNKS)):
+            for c in reversed(range(G)):
                 multiply(0, c, q)
+        w_interleave(act, 1)
 
         half = S // 2
         for c, j0, n in [(0, 0, 128), (0, 128, 128), (1, 0, half), (0, half, half), (1, half, half)]:

@@ -16,27 +16,32 @@ MULT = mybir.AluOpType.mult
 P = 128
 PACK = 4
 LIST = 16
-FIRST = 192
 CHUNKS = [(0, 256), (256, 128), (384, 128)]
+EARLY = 768
 
 
 def tile_list_hbag_none_kernel(tc, xT, w, wgt, offs, out):
     nc = tc.nc
     with ExitStack() as ctx:
         keep = ctx.enter_context(tc.tile_pool(name="keep", bufs=1))
+        reuse = ctx.enter_context(tc.tile_pool(name="reuse", bufs=1))
         psum = ctx.enter_context(tc.psum_pool(name="psum", bufs=1))
 
         offsets = keep.tile([P, G * S // LIST], U16, name="offsets")
         weights = keep.tile([P, G * S], F32, name="weights", align_bytes=64)
-        plane = [[keep.tile([P, T], F32, name=f"plane{a}_{i}", tag=f"plane{a}_{i}", align_bytes=64) for i in range(PACK)] for a in range(2)]
-        picked = [keep.tile([P, PACK, G * S], F32, name=f"picked{a}", tag=f"picked{a}", align_bytes=64) for a in range(2)]
-        first = keep.tile([P, 2, FIRST], F32, name="first", tag="first", align_bytes=64)
-        w_raw = [keep.tile([P, PACK, M], F32, name=f"w_raw{a}") for a in range(2)]
-        w_bf = [keep.tile([P, M, PACK], BF16, name=f"w_bf{a}", align_bytes=64) for a in range(2)]
-        w_codes = {}
-        w_scales = [keep.tile([P, M], U8, name=f"w_scales{a}", align_bytes=64) for a in range(2)]
-        x_bf = [keep.tile([P, G * S, PACK], BF16, name=f"x_bf{a}", align_bytes=64) for a in range(2)]
-        x_codes = [keep.tile([P, G * S], U32, name=f"x_codes{a}", align_bytes=64) for a in range(2)]
+        plane = [[keep.tile([P, T], F32, name=f"plane{a}_{i}", align_bytes=64) for i in range(PACK)] for a in range(2)]
+        picked0 = keep.tile([P, PACK, G * S], F32, name="picked0", align_bytes=64)
+        picked1 = keep.tile([P, 2, G * S], F32, name="picked1", align_bytes=64)
+        late = keep.tile([P, 4 * EARLY], F32, name="late", align_bytes=64)
+        w_raw = [
+            reuse.tile([P, PACK, M], F32, name="w_raw0", offset=2048, align_bytes=64),
+            keep.tile([P, PACK, M], F32, name="w_raw1", tag="w_raw1", align_bytes=64),
+        ]
+        w_bf = keep.tile([P, 2, M, PACK], BF16, name="w_bf", align_bytes=64)
+        w_codes = keep.tile([P, 2 * M], U32, name="w_codes", align_bytes=64)
+        w_scales = keep.tile([P, 2 * M], U8, name="w_scales", align_bytes=64)
+        x_bf0 = keep.tile([P, G * S, PACK], BF16, name="x_bf0", align_bytes=64)
+        x_codes = [None, keep.tile([P, G * S], U32, name="x_codes1", align_bytes=64)]
         x_scales = [keep.tile([P, G * S], U8, name=f"x_scales{a}", align_bytes=64) for a in range(2)]
         acc = [[psum.tile([P, n], F32, name=f"acc{j0}_{m}") for m in range(2)] for j0, n in CHUNKS]
         staged = [keep.tile([P, 2, n], F32, name=f"staged{j0}") for j0, n in CHUNKS]
@@ -48,70 +53,70 @@ def tile_list_hbag_none_kernel(tc, xT, w, wgt, offs, out):
         w_rows = w.rearrange("(a p i) n -> a p i n", a=2, i=PACK)
         out_rows = out.rearrange("(m p) j -> p m j", p=P)
 
+        act, dve = nc.scalar.copy, nc.vector.tensor_copy
+
         def load_plane(a, i):
             nc.sync.dma_start(out=plane[a][i][:], in_=x_rows[a, i])
 
         def load_w(a):
             nc.sync.dma_start(out=w_raw[a][:], in_=w_rows[a])
 
-        def lanes(a, h, e0, n):
-            if (a, h, e0) == (0, 1, 0):
-                return first[:]
-            return picked[a][:, 2 * h : 2 * h + 2, e0 : e0 + n]
-
-        def gather(a, i, e0=0, n=G * S):
+        def gather(dst, a, i, e0, n):
             nc.vector.tensor_tensor(
-                lanes(a, i // 2, e0, n)[:, i % 2],
+                dst,
                 plane[a][i][:].indirect(offsets[:, e0 // LIST : (e0 + n) // LIST]),
                 weights[:, e0 : e0 + n],
                 MULT,
             )
 
-        def column(a, c, q):
-            j0, n = CHUNKS[q]
-            return c * S + j0
+        def gather0(i, e0=0, n=G * S):
+            gather(picked0[:, i, e0 : e0 + n], 0, i, e0, n)
 
-        def w_interleave(copy, a):
-            copy(
-                w_bf[a][:].rearrange("p (u e) t -> p u t e", e=4),
+        def gather1(i, e0=0, n=G * S):
+            gather(picked1[:, i, e0 : e0 + n], 1, i, e0, n)
+
+        def slot(i, e0):
+            if i == 3:
+                return EARLY + e0
+            return e0 if e0 < EARLY else (e0 - EARLY) // P * EARLY
+
+        def gather_late(i, e0, n):
+            gather(late[:, slot(i, e0) : slot(i, e0) + n], 1, i, e0, n)
+
+        def pairs0(h, e0, n):
+            act(x_bf0[:, e0 : e0 + n, 2 * h : 2 * h + 2], picked0[:, 2 * h : 2 * h + 2, e0 : e0 + n].rearrange("p t j -> p j t"))
+
+        def late_pairs(e0, n):
+            c, j0 = divmod(e0, S)
+            lane2, lane3 = slot(2, e0), slot(3, e0)
+            lanes = late[:, lane2 : 2 * lane3 - lane2].rearrange("p (t j) -> p j t", t=2)
+            act(x_bf1[c][:, j0 : j0 + n, 2:4], lanes[:, 0:n, :])
+
+        def w_interleave(a):
+            act(
+                w_bf[:, a].rearrange("p (u e) t -> p u t e", e=4),
                 w_raw[a][:].rearrange("p t (u e) -> p u t e", e=4),
             )
 
-        def x_pairs(copy, a, h, e0, n):
-            copy(x_bf[a][:, e0 : e0 + n, 2 * h : 2 * h + 2], lanes(a, h, e0, n).rearrange("p t j -> p j t"))
+        def quantize(codes, scales, values):
+            nc.vector.quantize_mx(out=codes.bitcast(FP8X4), scales=scales, in_=values)
 
-        def x_interleave(copy, a, e0, n):
-            copy(
-                x_bf[a][:, e0 : e0 + n, :].rearrange("p (u e) t -> p u t e", e=4),
-                picked[a][:, :, e0 : e0 + n].rearrange("p t (u e) -> p u t e", e=4),
-            )
+        def quantize1(e0, n):
+            c, j0 = divmod(e0, S)
+            quantize(x_codes[1][:, e0 : e0 + n], x_scales[1][:, e0 : e0 + n], x_bf1[c][:, j0 : j0 + n, :].rearrange("p j t -> p (j t)"))
 
-        def x_quantize(a, col, n):
-            nc.vector.quantize_mx(
-                out=x_codes[a][:, col : col + n].bitcast(FP8X4),
-                scales=x_scales[a][:, col : col + n],
-                in_=x_bf[a][:, col : col + n, :].rearrange("p j t -> p (j t)"),
-            )
-
-        def w_quantize(a, after):
-            w_codes[a] = keep.tile([P, M], U32, name=f"w_codes{a}", tag=after, align_bytes=64)
-            nc.vector.quantize_mx(
-                out=w_codes[a][:].bitcast(FP8X4),
-                scales=w_scales[a][:],
-                in_=w_bf[a][:].rearrange("p n t -> p (n t)"),
-            )
-
-        def multiply(a, c, q, ms=(0, 1)):
-            n = CHUNKS[q][1]
-            col = column(a, c, q)
-            for m in ms:
+        def multiply(a, c, q):
+            j0, n = CHUNKS[q]
+            col = c * S + j0
+            for m in range(2):
+                w0 = a * M + m * P
                 nc.tensor.matmul_mx(
                     out=acc[q][m][:],
-                    lhsT=w_codes[a][:, m * P : (m + 1) * P].bitcast(FP8X4),
-                    lhsT_scale=w_scales[a][:, m * P : (m + 1) * P],
+                    lhsT=w_codes[:, w0 : w0 + P].bitcast(FP8X4),
+                    lhsT_scale=w_scales[:, w0 : w0 + P],
                     rhs=x_codes[a][:, col : col + n].bitcast(FP8X4),
                     rhs_scale=x_scales[a][:, col : col + n],
-                    start=(a == 0 and c == G - 1),
+                    start=(a == 0 and c == 0),
                     stop=(a == 1 and c == G - 1),
                 )
 
@@ -121,69 +126,72 @@ def tile_list_hbag_none_kernel(tc, xT, w, wgt, offs, out):
                 copies[m](staged[q][:, m, :], acc[q][m][:])
             nc.sync.dma_start(out=out_rows[:, :, j0 : j0 + n], in_=staged[q][:])
 
-        act, dve = nc.scalar.copy, nc.vector.tensor_copy
-
         wgt_rows = wgt.rearrange("(g r) (b s) -> r g b s", r=LIST, s=64)
         nc.sync.dma_start(out=w_rows32[:].rearrange("p u s -> p (u s)"), in_=wgt_rows[0])
-        load_plane(1, 0)
+        load_plane(0, 0)
         nc.sync.dma_start(offsets[:], offs)
-        load_plane(1, 1)
-        for i in range(3):
+        for i in range(1, PACK):
             load_plane(0, i)
+        load_plane(1, 0)
+        load_plane(1, 1)
         load_w(0)
-        load_plane(0, 3)
         load_plane(1, 2)
         load_w(1)
         load_plane(1, 3)
 
         for h in range(2):
             nc.vector.transpose(w_cols32[:, h, :], w_rows32[:, h, :])
-        for c, copy in enumerate((dve, dve)):
-            copy(
+        for c in range(G):
+            dve(
                 w_spread[c][:],
                 w_cols32[:].rearrange("p u (h b) -> p b u h", h=2)[:, 8 * c : 8 * (c + 1)].unsqueeze(4).to_broadcast([P, 8, 2, 2, 16]),
             )
         for c in range(G):
             nc.vector.transpose(weights[:, c * S : (c + 1) * S], w_spread[c][:].rearrange("p b u h r -> p (b u h r)"))
 
+        gather0(0)
+        gather0(1)
+        pairs0(0, 0, G * S)
+        gather0(2)
         for c in range(G):
-            gather(1, 0, c * S, S)
-        gather(1, 1)
-        x_pairs(act, 1, 0, 0, G * S)
-        gather(0, 0)
-        gather(0, 1)
-        x_pairs(act, 0, 0, 0, S)
-        gather(0, 2, 0, FIRST)
-        gather(0, 2, FIRST, G * S - FIRST)
-        w_interleave(act, 0)
-        for e0, n in ((0, 192), (192, 320)):
-            gather(0, 3, e0, n)
-            x_pairs(act, 0, 1, e0, n)
-        gather(0, 3, S, S)
-        x_interleave(act, 0, S, S)
-        w_quantize(0, "first")
-        x_quantize(0, 0, S)
-        gather(1, 2)
-        x_quantize(0, S, S)
-        for q in range(len(CHUNKS)):
-            for c in reversed(range(G)):
+            gather0(3, c * S, S)
+            pairs0(1, c * S, S)
+        gather1(0)
+        for c in range(G):
+            gather1(1, c * S, S)
+        w_interleave(0)
+        x_codes[0] = reuse.tile([P, G * S], U32, name="x_codes0", offset=0, align_bytes=64)
+        quantize(x_codes[0][:], x_scales[0][:], x_bf0[:].rearrange("p j t -> p (j t)"))
+        x_bf1 = [reuse.tile([P, S, PACK], BF16, name="x_bf1_0", offset=4096, align_bytes=64)]
+        act(x_bf1[0][:, :, 0:2], picked1[:, :, 0:S].rearrange("p t j -> p j t"))
+        gather_late(2, 0, EARLY)
+        w_interleave(1)
+        x_bf1.append(keep.tile([P, S, PACK], BF16, name="x_bf1_1", tag="w_raw1", align_bytes=64))
+        act(x_bf1[1][:, :, 0:2], picked1[:, :, S : G * S].rearrange("p t j -> p j t"))
+        quantize(w_codes[:], w_scales[:], w_bf[:].rearrange("p a n t -> p (a n t)"))
+        for c in range(G):
+            for q in range(len(CHUNKS)):
                 multiply(0, c, q)
-        w_interleave(act, 1)
 
+        for e0, n in ((0, 128), (128, 128), (512, 256), (256, 256)):
+            gather_late(3, e0, n)
+            late_pairs(e0, n)
+        gather_late(3, 768, 256)
+        for e0 in (768, 896):
+            gather_late(2, e0, 128)
+            late_pairs(e0, 128)
+        for c in range(G):
+            quantize1(c * S, 256)
+            multiply(1, c, 0)
+        quantize1(256, 256)
+        for q in (1, 2):
+            multiply(1, 0, q)
+        for q in (1, 2):
+            quantize1(S + CHUNKS[q][0], 128)
+            multiply(1, 1, q)
         half = S // 2
-        for c, j0, n in [(0, 0, 128), (0, 128, 128), (1, 0, half), (0, half, half), (1, half, half)]:
-            gather(1, 3, c * S + j0, n)
-        pieces = [(0, 0, half, (0,)), (1, 0, half, (0,)), (0, half, half, (1, 2)), (1, *CHUNKS[1], (1,)), (1, *CHUNKS[2], (2,))]
-        for c, j0, n in [(0, 0, 128), (0, 128, 128)] + [piece[:3] for piece in pieces[1:]]:
-            x_pairs(act, 1, 1, c * S + j0, n)
-        for number, (c, j0, n, chunks) in enumerate(pieces):
-            x_quantize(1, c * S + j0, n)
-            if number == 0:
-                w_quantize(1, "plane1_3")
-            for q in chunks:
-                multiply(1, c, q)
         for m in range(2):
             act(staged[0][:, m, :], acc[0][m][:])
             nc.sync.dma_start(out=out_rows[:, m, 0:half], in_=staged[0][:, m, :])
-        store(1, (dve, dve))
+        store(1, (dve, act))
         store(2, (dve, act))

@@ -18,6 +18,7 @@ PACK = 4
 LIST = 16
 CHUNKS = [(0, 256), (256, 128), (384, 128)]
 EARLY = 768
+ODD_AT, WEIGHTS_AT, PICKED_AT = 56 * 1024, 112 * 1024, 150 * 1024
 
 
 def tile_list_hbag_none_kernel(tc, xT, w, wgt, offs, out):
@@ -25,14 +26,21 @@ def tile_list_hbag_none_kernel(tc, xT, w, wgt, offs, out):
     with ExitStack() as ctx:
         keep = ctx.enter_context(tc.tile_pool(name="keep", bufs=1))
         reuse = ctx.enter_context(tc.tile_pool(name="reuse", bufs=1))
+        laid = ctx.enter_context(tc.tile_pool(name="laid", bufs=1))
         psum = ctx.enter_context(tc.psum_pool(name="psum", bufs=1))
 
         offsets = keep.tile([P, G * S // LIST], U16, name="offsets")
-        weights = keep.tile([P, G * S], F32, name="weights", align_bytes=64)
-        plane = [[keep.tile([P, T], F32, name=f"plane{a}_{i}", align_bytes=64) for i in range(PACK)] for a in range(2)]
-        picked0 = keep.tile([P, PACK, G * S], F32, name="picked0", align_bytes=64)
-        picked1 = keep.tile([P, 2, G * S], F32, name="picked1", align_bytes=64)
-        late = keep.tile([P, 4 * EARLY], F32, name="late", align_bytes=64)
+        weights = laid.tile([P, G * S], F32, name="weights", offset=WEIGHTS_AT, align_bytes=64)
+        plane = [
+            [
+                laid.tile([P, T], F32, name=f"plane{a}_{i}", offset=(i % 2) * ODD_AT + (2 * a + i // 2) * 4 * T, align_bytes=64)
+                for i in range(PACK)
+            ]
+            for a in range(2)
+        ]
+        picked0 = laid.tile([P, PACK, G * S], F32, name="picked0", offset=PICKED_AT, align_bytes=64)
+        picked1 = laid.tile([P, 2, G * S], F32, name="picked1", offset=PICKED_AT + 16384, align_bytes=64)
+        late = laid.tile([P, 4 * EARLY], F32, name="late", offset=PICKED_AT + 24576, align_bytes=64)
         w_raw = [
             reuse.tile([P, PACK, M], F32, name="w_raw0", offset=2048, align_bytes=64),
             keep.tile([P, PACK, M], F32, name="w_raw1", tag="w_raw1", align_bytes=64),

@@ -30,33 +30,33 @@ def tile_list_hbag_none_kernel(tc, xT, w, wgt, offs, out):
         psum = ctx.enter_context(tc.psum_pool(name="psum", bufs=1))
 
         offsets = keep.tile([P, G * S // LIST], U16, name="offsets")
-        weights = laid.tile([P, G * S], F32, name="weights", offset=WEIGHTS_AT, align_bytes=64)
+        weights = laid.tile([P, G * S], F32, name="weights", offset=WEIGHTS_AT, align_bytes=256)
         plane = [
             [
-                laid.tile([P, T], F32, name=f"plane{a}_{i}", offset=(i % 2) * ODD_AT + (2 * a + i // 2) * 4 * T, align_bytes=64)
+                laid.tile([P, T], F32, name=f"plane{a}_{i}", offset=(i % 2) * ODD_AT + (2 * a + i // 2) * 4 * T, align_bytes=256)
                 for i in range(PACK)
             ]
             for a in range(2)
         ]
-        picked0 = laid.tile([P, PACK, G * S], F32, name="picked0", offset=PICKED_AT, align_bytes=64)
-        picked1 = laid.tile([P, 2, G * S], F32, name="picked1", offset=PICKED_AT + 16384, align_bytes=64)
-        late = laid.tile([P, 4 * EARLY], F32, name="late", offset=PICKED_AT + 24576, align_bytes=64)
+        picked0 = laid.tile([P, PACK, G * S], F32, name="picked0", offset=PICKED_AT, align_bytes=256)
+        picked1 = laid.tile([P, 2, G * S], F32, name="picked1", offset=PICKED_AT + 16384, align_bytes=256)
+        late = laid.tile([P, 4 * EARLY], F32, name="late", offset=PICKED_AT + 24576, align_bytes=256)
         w_raw = [
-            reuse.tile([P, PACK, M], F32, name="w_raw0", offset=2048, align_bytes=64),
-            keep.tile([P, PACK, M], F32, name="w_raw1", tag="w_raw1", align_bytes=64),
+            reuse.tile([P, PACK, M], F32, name="w_raw0", offset=2048, align_bytes=256),
+            keep.tile([P, PACK, M], F32, name="w_raw1", tag="w_raw1", align_bytes=256),
         ]
-        w_bf = keep.tile([P, 2, M, PACK], BF16, name="w_bf", align_bytes=64)
-        w_codes = keep.tile([P, 2 * M], U32, name="w_codes", align_bytes=64)
-        w_scales = keep.tile([P, 2 * M], U8, name="w_scales", align_bytes=64)
-        x_bf0 = keep.tile([P, G * S, PACK], BF16, name="x_bf0", align_bytes=64)
-        x_codes = [None, keep.tile([P, G * S], U32, name="x_codes1", align_bytes=64)]
-        x_scales = [keep.tile([P, G * S], U8, name=f"x_scales{a}", align_bytes=64) for a in range(2)]
+        w_bf = keep.tile([P, 2, M, PACK], BF16, name="w_bf", align_bytes=256)
+        w_codes = keep.tile([P, 2 * M], U32, name="w_codes", align_bytes=256)
+        w_scales = keep.tile([P, 2 * M], U8, name="w_scales", align_bytes=256)
+        x_bf0 = keep.tile([P, G * S, PACK], BF16, name="x_bf0", align_bytes=256)
+        x_codes = [None, keep.tile([P, G * S], U32, name="x_codes1", align_bytes=256)]
+        x_scales = [keep.tile([P, G * S], U8, name=f"x_scales{a}", align_bytes=256) for a in range(2)]
         acc = [[psum.tile([P, n], F32, name=f"acc{j0}_{m}") for m in range(2)] for j0, n in CHUNKS]
-        staged = [keep.tile([P, 2, n], F32, name=f"staged{j0}") for j0, n in CHUNKS]
+        staged = [keep.tile([P, 2, n], F32, name=f"staged{j0}", align_bytes=256) for j0, n in CHUNKS]
 
-        w_rows32 = keep.tile([P, 2, 32], F32, name="wgt_rows", align_bytes=64)
-        w_cols32 = keep.tile([P, 2, 32], F32, name="wgt_cols", align_bytes=64)
-        w_spread = [keep.tile([P, 8, 2, 2, 16], F32, name=f"wgt_spread{c}", align_bytes=64) for c in range(G)]
+        w_rows32 = keep.tile([P, 2, 32], F32, name="wgt_rows", align_bytes=256)
+        w_cols32 = keep.tile([P, 2, 32], F32, name="wgt_cols", align_bytes=256)
+        w_spread = [keep.tile([P, 8, 2, 2, 16], F32, name=f"wgt_spread{c}", align_bytes=256) for c in range(G)]
         x_rows = xT.rearrange("(a p i) t -> a i p t", a=2, i=PACK)
         w_rows = w.rearrange("(a p i) n -> a p i n", a=2, i=PACK)
         out_rows = out.rearrange("(m p) j -> p m j", p=P)
@@ -168,13 +168,13 @@ def tile_list_hbag_none_kernel(tc, xT, w, wgt, offs, out):
         for c in range(G):
             gather1(1, c * S, S)
         w_interleave(0)
-        x_codes[0] = reuse.tile([P, G * S], U32, name="x_codes0", offset=0, align_bytes=64)
+        x_codes[0] = reuse.tile([P, G * S], U32, name="x_codes0", offset=0, align_bytes=256)
         quantize(x_codes[0][:], x_scales[0][:], x_bf0[:].rearrange("p j t -> p (j t)"))
-        x_bf1 = [reuse.tile([P, S, PACK], BF16, name="x_bf1_0", offset=4096, align_bytes=64)]
+        x_bf1 = [reuse.tile([P, S, PACK], BF16, name="x_bf1_0", offset=4096, align_bytes=256)]
         act(x_bf1[0][:, :, 0:2], picked1[:, :, 0:S].rearrange("p t j -> p j t"))
         gather_late(2, 0, EARLY)
         w_interleave(1)
-        x_bf1.append(keep.tile([P, S, PACK], BF16, name="x_bf1_1", tag="w_raw1", align_bytes=64))
+        x_bf1.append(keep.tile([P, S, PACK], BF16, name="x_bf1_1", tag="w_raw1", align_bytes=256))
         act(x_bf1[1][:, :, 0:2], picked1[:, :, S : G * S].rearrange("p t j -> p j t"))
         quantize(w_codes[:], w_scales[:], w_bf[:].rearrange("p a n t -> p (a n t)"))
         for c in range(G):

@@ -52,7 +52,7 @@ def tile_list_hbag_none_kernel(tc, xT, w, wgt, offs, out):
         x_codes = [None, keep.tile([P, G * S], U32, name="x_codes1", align_bytes=256)]
         x_scales = [keep.tile([P, G * S], U8, name=f"x_scales{a}", align_bytes=256) for a in range(2)]
         acc = [[psum.tile([P, n], F32, name=f"acc{j0}_{m}") for m in range(2)] for j0, n in CHUNKS]
-        staged = [keep.tile([P, 2, n], F32, name=f"staged{j0}", align_bytes=256) for j0, n in CHUNKS]
+        staged = [keep.tile([P, S], F32, name=f"staged{m}", align_bytes=256) for m in range(2)]
 
         w_rows32 = keep.tile([P, 2, 32], F32, name="wgt_rows", align_bytes=256)
         w_cols32 = keep.tile([P, 2, 32], F32, name="wgt_cols", align_bytes=256)
@@ -128,11 +128,12 @@ def tile_list_hbag_none_kernel(tc, xT, w, wgt, offs, out):
                     stop=(a == 1 and c == G - 1),
                 )
 
-        def store(q, copies):
+        def leave(copy, q, m):
             j0, n = CHUNKS[q]
-            for m in range(2):
-                copies[m](staged[q][:, m, :], acc[q][m][:])
-            nc.sync.dma_start(out=out_rows[:, :, j0 : j0 + n], in_=staged[q][:])
+            copy(staged[m][:, j0 : j0 + n], acc[q][m][:])
+
+        def store(m, j0, n):
+            nc.sync.dma_start(out=out_rows[:, m, j0 : j0 + n], in_=staged[m][:, j0 : j0 + n])
 
         wgt_rows = wgt.rearrange("(g r) (b s) -> r g b s", r=LIST, s=64)
         nc.sync.dma_start(out=w_rows32[:].rearrange("p u s -> p (u s)"), in_=wgt_rows[0])
@@ -199,7 +200,10 @@ def tile_list_hbag_none_kernel(tc, xT, w, wgt, offs, out):
             multiply(1, 1, q)
         half = S // 2
         for m in range(2):
-            act(staged[0][:, m, :], acc[0][m][:])
-            nc.sync.dma_start(out=out_rows[:, m, 0:half], in_=staged[0][:, m, :])
-        store(1, (dve, act))
-        store(2, (dve, act))
+            leave(act, 0, m)
+            store(m, 0, half)
+        for q in (1, 2):
+            leave(dve, q, 0)
+            leave(act, q, 1)
+        for m in range(2):
+            store(m, half, half)

@@ -18,7 +18,8 @@ PACK = 4
 LIST = 16
 CHUNKS = [(0, 256), (256, 128), (384, 128)]
 EARLY = 768
-ODD_AT, WEIGHTS_AT, PICKED_AT = 56 * 1024, 112 * 1024, 150 * 1024
+LAST = 896
+ODD_AT, WEIGHTS_AT, PICKED_AT = 56 * 1024, 112 * 1024, 148 * 1024
 
 
 def tile_list_hbag_none_kernel(tc, xT, w, wgt, offs, out):
@@ -94,8 +95,17 @@ def tile_list_hbag_none_kernel(tc, xT, w, wgt, offs, out):
         def pairs0(h, e0, n):
             act(x_bf0[:, e0 : e0 + n, 2 * h : 2 * h + 2], picked0[:, 2 * h : 2 * h + 2, e0 : e0 + n].rearrange("p t j -> p j t"))
 
+        def part(e0):
+            if S <= e0 < LAST:
+                return 1, e0 - S
+            return 0, e0 if e0 < S else e0 - LAST + S
+
+        def early_pairs(e0, n):
+            c, j0 = part(e0)
+            act(x_bf1[c][:, j0 : j0 + n, 0:2], picked1[:, :, e0 : e0 + n].rearrange("p t j -> p j t"))
+
         def late_pairs(e0, n):
-            c, j0 = divmod(e0, S)
+            c, j0 = part(e0)
             lane2, lane3 = slot(2, e0), slot(3, e0)
             lanes = late[:, lane2 : 2 * lane3 - lane2].rearrange("p (t j) -> p j t", t=2)
             act(x_bf1[c][:, j0 : j0 + n, 2:4], lanes[:, 0:n, :])
@@ -110,7 +120,7 @@ def tile_list_hbag_none_kernel(tc, xT, w, wgt, offs, out):
             nc.vector.quantize_mx(out=codes.bitcast(FP8X4), scales=scales, in_=values)
 
         def quantize1(e0, n):
-            c, j0 = divmod(e0, S)
+            c, j0 = part(e0)
             quantize(x_codes[1][:, e0 : e0 + n], x_scales[1][:, e0 : e0 + n], x_bf1[c][:, j0 : j0 + n, :].rearrange("p j t -> p (j t)"))
 
         def multiply(a, c, q):
@@ -171,12 +181,13 @@ def tile_list_hbag_none_kernel(tc, xT, w, wgt, offs, out):
         w_interleave(0)
         x_codes[0] = reuse.tile([P, G * S], U32, name="x_codes0", offset=0, align_bytes=256)
         quantize(x_codes[0][:], x_scales[0][:], x_bf0[:].rearrange("p j t -> p (j t)"))
-        x_bf1 = [reuse.tile([P, S, PACK], BF16, name="x_bf1_0", offset=4096, align_bytes=256)]
-        act(x_bf1[0][:, :, 0:2], picked1[:, :, 0:S].rearrange("p t j -> p j t"))
+        x_bf1 = [reuse.tile([P, S + G * S - LAST, PACK], BF16, name="x_bf1_0", offset=4096, align_bytes=256)]
+        early_pairs(0, S)
+        early_pairs(LAST, G * S - LAST)
         gather_late(2, 0, EARLY)
         w_interleave(1)
-        x_bf1.append(keep.tile([P, S, PACK], BF16, name="x_bf1_1", tag="w_raw1", align_bytes=256))
-        act(x_bf1[1][:, :, 0:2], picked1[:, :, S : G * S].rearrange("p t j -> p j t"))
+        x_bf1.append(keep.tile([P, LAST - S, PACK], BF16, name="x_bf1_1", tag="w_raw1", align_bytes=256))
+        early_pairs(S, LAST - S)
         quantize(w_codes[:], w_scales[:], w_bf[:].rearrange("p a n t -> p (a n t)"))
         for c in range(G):
             for q in range(len(CHUNKS)):

@@ -19,6 +19,7 @@ LIST = 16
 CHUNKS = [(0, 256), (256, 128), (384, 128)]
 EARLY = 768
 LAST = 896
+WARM = 3
 ODD_AT, WEIGHTS_AT, PICKED_AT = 56 * 1024, 112 * 1024, 148 * 1024
 
 
@@ -192,6 +193,17 @@ def tile_list_hbag_none_kernel(tc, xT, w, wgt, offs, out):
         for c in range(G):
             for q in range(len(CHUNKS)):
                 multiply(0, c, q)
+        unread = psum.tile([P, WARM, P], F32, name="unread")
+        for u in range(WARM):
+            nc.tensor.matmul_mx(
+                out=unread[:, u, :],
+                lhsT=w_codes[:, 0:P].bitcast(FP8X4),
+                lhsT_scale=w_scales[:, 0:P],
+                rhs=x_codes[0][:, 0:P].bitcast(FP8X4),
+                rhs_scale=x_scales[0][:, 0:P],
+                start=True,
+                stop=True,
+            )
 
         for e0, n in ((0, 128), (128, 128), (512, 256), (256, 256)):
             gather_late(3, e0, n)

@@ -16,9 +16,11 @@ MULT = mybir.AluOpType.mult
 P = 128
 PACK = 4
 LIST = 16
+E = G * S
 CHUNKS = [(0, 256), (256, 128), (384, 128)]
+PAIRED = 768
 EARLY = 768
-LAST = 896
+FIRST = 192
 WARM = 3
 ODD_AT, WEIGHTS_AT, PICKED_AT = 56 * 1024, 112 * 1024, 148 * 1024
 
@@ -31,8 +33,8 @@ def tile_list_hbag_none_kernel(tc, xT, w, wgt, offs, out):
         laid = ctx.enter_context(tc.tile_pool(name="laid", bufs=1))
         psum = ctx.enter_context(tc.psum_pool(name="psum", bufs=1))
 
-        offsets = keep.tile([P, G * S // LIST], U16, name="offsets")
-        weights = laid.tile([P, G * S], F32, name="weights", offset=WEIGHTS_AT, align_bytes=256)
+        offsets = keep.tile([P, E // LIST], U16, name="offsets")
+        weights = laid.tile([P, E], F32, name="weights", offset=WEIGHTS_AT, align_bytes=256)
         plane = [
             [
                 laid.tile([P, T], F32, name=f"plane{a}_{i}", offset=(i % 2) * ODD_AT + (2 * a + i // 2) * 4 * T, align_bytes=256)
@@ -40,19 +42,19 @@ def tile_list_hbag_none_kernel(tc, xT, w, wgt, offs, out):
             ]
             for a in range(2)
         ]
-        picked0 = laid.tile([P, PACK, G * S], F32, name="picked0", offset=PICKED_AT, align_bytes=256)
-        picked1 = laid.tile([P, 2, G * S], F32, name="picked1", offset=PICKED_AT + 16384, align_bytes=256)
-        late = laid.tile([P, 4 * EARLY], F32, name="late", offset=PICKED_AT + 24576, align_bytes=256)
+        picked0 = laid.tile([P, PACK, E], F32, name="picked0", offset=PICKED_AT, align_bytes=256)
+        picked1 = laid.tile([P, 2, E], F32, name="picked1", offset=PICKED_AT + 16384, align_bytes=256)
+        late = laid.tile([P, 2 * (EARLY + FIRST) + E - FIRST], F32, name="late", offset=PICKED_AT + 24576, align_bytes=256)
         w_raw = [
-            reuse.tile([P, PACK, M], F32, name="w_raw0", offset=2048, align_bytes=256),
-            keep.tile([P, PACK, M], F32, name="w_raw1", tag="w_raw1", align_bytes=256),
+            reuse.tile([P, PACK, M], F32, name="w_raw0", offset=0, align_bytes=256),
+            keep.tile([P, PACK, M], F32, name="w_raw1", align_bytes=256),
         ]
-        w_bf = keep.tile([P, 2, M, PACK], BF16, name="w_bf", align_bytes=256)
-        w_codes = keep.tile([P, 2 * M], U32, name="w_codes", align_bytes=256)
-        w_scales = keep.tile([P, 2 * M], U8, name="w_scales", align_bytes=256)
-        x_bf0 = keep.tile([P, G * S, PACK], BF16, name="x_bf0", align_bytes=256)
-        x_codes = [None, keep.tile([P, G * S], U32, name="x_codes1", align_bytes=256)]
-        x_scales = [keep.tile([P, G * S], U8, name=f"x_scales{a}", align_bytes=256) for a in range(2)]
+        w_bf = [keep.tile([P, M, PACK], BF16, name=f"w_bf{a}", align_bytes=256) for a in range(2)]
+        w_codes = [keep.tile([P, M], U32, name=f"w_codes{a}", align_bytes=256) for a in range(2)]
+        w_scales = [keep.tile([P, M], U8, name=f"w_scales{a}", align_bytes=256) for a in range(2)]
+        x_bf0 = keep.tile([P, PAIRED, PACK], BF16, name="x_bf0", align_bytes=256)
+        x_codes = [None, keep.tile([P, E], U32, name="x_codes1", align_bytes=256)]
+        x_scales = [keep.tile([P, E], U8, name=f"x_scales{a}", align_bytes=256) for a in range(2)]
         acc = [[psum.tile([P, n], F32, name=f"acc{j0}_{m}") for m in range(2)] for j0, n in CHUNKS]
         staged = [keep.tile([P, S], F32, name=f"staged{m}", align_bytes=256) for m in range(2)]
 
@@ -79,16 +81,11 @@ def tile_list_hbag_none_kernel(tc, xT, w, wgt, offs, out):
                 MULT,
             )
 
-        def gather0(i, e0=0, n=G * S):
-            gather(picked0[:, i, e0 : e0 + n], 0, i, e0, n)
-
-        def gather1(i, e0=0, n=G * S):
-            gather(picked1[:, i, e0 : e0 + n], 1, i, e0, n)
-
         def slot(i, e0):
-            if i == 3:
-                return EARLY + e0
-            return e0 if e0 < EARLY else (e0 - EARLY) // P * EARLY
+            two = e0 if e0 < EARLY else e0 - FIRST
+            if i == 2:
+                return two
+            return two + (FIRST if EARLY - FIRST <= e0 < EARLY else EARLY + FIRST)
 
         def gather_late(i, e0, n):
             gather(late[:, slot(i, e0) : slot(i, e0) + n], 1, i, e0, n)
@@ -96,47 +93,37 @@ def tile_list_hbag_none_kernel(tc, xT, w, wgt, offs, out):
         def pairs0(h, e0, n):
             act(x_bf0[:, e0 : e0 + n, 2 * h : 2 * h + 2], picked0[:, 2 * h : 2 * h + 2, e0 : e0 + n].rearrange("p t j -> p j t"))
 
-        def part(e0):
-            if S <= e0 < LAST:
-                return 1, e0 - S
-            return 0, e0 if e0 < S else e0 - LAST + S
+        def four_lanes(dst, src):
+            act(dst.rearrange("p (u e) t -> p u t e", e=4), src.rearrange("p t (u e) -> p u t e", e=4))
 
-        def early_pairs(e0, n):
-            c, j0 = part(e0)
-            act(x_bf1[c][:, j0 : j0 + n, 0:2], picked1[:, :, e0 : e0 + n].rearrange("p t j -> p j t"))
+        def early_pairs(c):
+            act(x_bf1[c][:, :, 0:2], picked1[:, :, c * S : (c + 1) * S].rearrange("p t j -> p j t"))
 
         def late_pairs(e0, n):
-            c, j0 = part(e0)
+            c, j0 = divmod(e0, S)
             lane2, lane3 = slot(2, e0), slot(3, e0)
-            lanes = late[:, lane2 : 2 * lane3 - lane2].rearrange("p (t j) -> p j t", t=2)
-            act(x_bf1[c][:, j0 : j0 + n, 2:4], lanes[:, 0:n, :])
-
-        def w_interleave(a):
-            act(
-                w_bf[:, a].rearrange("p (u e) t -> p u t e", e=4),
-                w_raw[a][:].rearrange("p t (u e) -> p u t e", e=4),
-            )
+            step = lane3 - lane2
+            act(x_bf1[c][:, j0 : j0 + n, 2:4], late[:, lane2 : lane2 + 2 * step].rearrange("p (t j) -> p j t", t=2)[:, 0:n, :])
 
         def quantize(codes, scales, values):
-            nc.vector.quantize_mx(out=codes.bitcast(FP8X4), scales=scales, in_=values)
+            nc.vector.quantize_mx(out=codes.bitcast(FP8X4), scales=scales, in_=values.rearrange("p j t -> p (j t)"))
 
         def quantize1(e0, n):
-            c, j0 = part(e0)
-            quantize(x_codes[1][:, e0 : e0 + n], x_scales[1][:, e0 : e0 + n], x_bf1[c][:, j0 : j0 + n, :].rearrange("p j t -> p (j t)"))
+            c, j0 = divmod(e0, S)
+            quantize(x_codes[1][:, e0 : e0 + n], x_scales[1][:, e0 : e0 + n], x_bf1[c][:, j0 : j0 + n, :])
 
-        def multiply(a, c, q):
+        def multiply(a, c, q, start, stop):
             j0, n = CHUNKS[q]
             col = c * S + j0
             for m in range(2):
-                w0 = a * M + m * P
                 nc.tensor.matmul_mx(
                     out=acc[q][m][:],
-                    lhsT=w_codes[:, w0 : w0 + P].bitcast(FP8X4),
-                    lhsT_scale=w_scales[:, w0 : w0 + P],
+                    lhsT=w_codes[a][:, m * P : (m + 1) * P].bitcast(FP8X4),
+                    lhsT_scale=w_scales[a][:, m * P : (m + 1) * P],
                     rhs=x_codes[a][:, col : col + n].bitcast(FP8X4),
                     rhs_scale=x_scales[a][:, col : col + n],
-                    start=(a == 0 and c == 0),
-                    stop=(a == 1 and c == G - 1),
+                    start=start,
+                    stop=stop,
                 )
 
         def leave(copy, q, m):
@@ -152,11 +139,10 @@ def tile_list_hbag_none_kernel(tc, xT, w, wgt, offs, out):
         nc.sync.dma_start(offsets[:], offs)
         for i in range(1, PACK):
             load_plane(0, i)
-        load_plane(1, 0)
-        load_plane(1, 1)
-        load_w(0)
-        load_plane(1, 2)
         load_w(1)
+        for i in range(3):
+            load_plane(1, i)
+        load_w(0)
         load_plane(1, 3)
 
         for h in range(2):
@@ -169,58 +155,65 @@ def tile_list_hbag_none_kernel(tc, xT, w, wgt, offs, out):
         for c in range(G):
             nc.vector.transpose(weights[:, c * S : (c + 1) * S], w_spread[c][:].rearrange("p b u h r -> p (b u h r)"))
 
-        gather0(0)
-        gather0(1)
-        pairs0(0, 0, G * S)
-        gather0(2)
+        for i in range(PACK):
+            gather(picked0[:, i, :], 0, i, 0, E)
+            if i == 1:
+                pairs0(0, 0, PAIRED)
+        four_lanes(w_bf[1][:], w_raw[1][:])
+        quantize(w_codes[1][:], w_scales[1][:], w_bf[1][:])
+        pairs0(1, 0, PAIRED)
+        gather(picked1[:, 0, :], 1, 0, 0, E)
+        x_bf0_end = laid.tile([P, E - PAIRED, PACK], BF16, name="x_bf0_end", offset=2 * 4 * T, align_bytes=256)
+        four_lanes(x_bf0_end[:], picked0[:, :, PAIRED:E])
         for c in range(G):
-            gather0(3, c * S, S)
-            pairs0(1, c * S, S)
-        gather1(0)
-        for c in range(G):
-            gather1(1, c * S, S)
-        w_interleave(0)
-        x_codes[0] = reuse.tile([P, G * S], U32, name="x_codes0", offset=0, align_bytes=256)
-        quantize(x_codes[0][:], x_scales[0][:], x_bf0[:].rearrange("p j t -> p (j t)"))
-        x_bf1 = [reuse.tile([P, S + G * S - LAST, PACK], BF16, name="x_bf1_0", offset=4096, align_bytes=256)]
-        early_pairs(0, S)
-        early_pairs(LAST, G * S - LAST)
+            gather(picked1[:, 1, c * S : (c + 1) * S], 1, 1, c * S, S)
+        x_codes[0] = laid.tile([P, E], U32, name="x_codes0", offset=PICKED_AT, align_bytes=256)
+        for e0, e1 in ((0, S), (S, PAIRED)):
+            quantize(x_codes[0][:, e0:e1], x_scales[0][:, e0:e1], x_bf0[:, e0:e1, :])
+        quantize(x_codes[0][:, PAIRED:E], x_scales[0][:, PAIRED:E], x_bf0_end[:])
+        x_bf1 = [keep.tile([P, S, PACK], BF16, name="x_bf1_0", align_bytes=256)]
+        early_pairs(0)
         gather_late(2, 0, EARLY)
-        w_interleave(1)
-        x_bf1.append(keep.tile([P, LAST - S, PACK], BF16, name="x_bf1_1", tag="w_raw1", align_bytes=256))
-        early_pairs(S, LAST - S)
-        quantize(w_codes[:], w_scales[:], w_bf[:].rearrange("p a n t -> p (a n t)"))
+        four_lanes(w_bf[0][:], w_raw[0][:])
+        x_bf1.append(reuse.tile([P, S, PACK], BF16, name="x_bf1_1", offset=0, align_bytes=256))
+        early_pairs(1)
+        quantize(w_codes[0][:], w_scales[0][:], w_bf[0][:])
         for c in range(G):
             for q in range(len(CHUNKS)):
-                multiply(0, c, q)
+                multiply(0, c, q, c == 0, False)
         unread = psum.tile([P, WARM, P], F32, name="unread")
         for u in range(WARM):
             nc.tensor.matmul_mx(
                 out=unread[:, u, :],
-                lhsT=w_codes[:, 0:P].bitcast(FP8X4),
-                lhsT_scale=w_scales[:, 0:P],
+                lhsT=w_codes[0][:, 0:P].bitcast(FP8X4),
+                lhsT_scale=w_scales[0][:, 0:P],
                 rhs=x_codes[0][:, 0:P].bitcast(FP8X4),
                 rhs_scale=x_scales[0][:, 0:P],
                 start=True,
                 stop=True,
             )
 
-        for e0, n in ((0, 128), (128, 128), (512, 256), (256, 256)):
-            gather_late(3, e0, n)
-            late_pairs(e0, n)
-        gather_late(3, 768, 256)
-        for e0 in (768, 896):
+        head = EARLY - FIRST
+        gather_late(3, head, FIRST)
+        late_pairs(head, FIRST)
+        gather_late(3, 0, 256)
+        late_pairs(0, 256)
+        gather_late(3, 256, head - 256)
+        late_pairs(S, head - S)
+        late_pairs(256, 256)
+        gather_late(3, EARLY, E - EARLY)
+        for e0 in (EARLY, EARLY + 128):
             gather_late(2, e0, 128)
             late_pairs(e0, 128)
         for c in range(G):
             quantize1(c * S, 256)
-            multiply(1, c, 0)
+            multiply(1, c, 0, False, c == 1)
         quantize1(256, 256)
         for q in (1, 2):
-            multiply(1, 0, q)
+            multiply(1, 0, q, False, False)
         for q in (1, 2):
             quantize1(S + CHUNKS[q][0], 128)
-            multiply(1, 1, q)
+            multiply(1, 1, q, False, True)
         half = S // 2
         for m in range(2):
             leave(act, 0, m)

@@ -133,8 +133,8 @@ def tile_list_hbag_none_kernel(tc, xT, w, wgt, offs, out):
         def store(m, j0, n):
             nc.sync.dma_start(out=out_rows[:, m, j0 : j0 + n], in_=staged[m][:, j0 : j0 + n])
 
-        wgt_rows = wgt.rearrange("(g r) (b s) -> r g b s", r=LIST, s=64)
-        nc.sync.dma_start(out=w_rows32[:].rearrange("p u s -> p (u s)"), in_=wgt_rows[0])
+        wgt_halves = wgt.rearrange("p (c s) -> (p c) s", c=G)[0 : P * G : LIST + 1]
+        nc.sync.dma_start(out=w_rows32[:].rearrange("p u s -> p (u s)"), in_=wgt_halves.rearrange("u (b s) -> u b s", s=64))
         load_plane(0, 0)
         nc.sync.dma_start(offsets[:], offs)
         for i in range(1, PACK):

@@ -17,24 +17,25 @@ P = 128
 PACK = 4
 LIST = 16
 E = G * S
-CHUNKS = [(0, 256), (256, 128), (384, 128)]
+A, B, C = (0, 256), (256, 128), (384, 128)
 PAIRED = 768
 EARLY = 768
-FIRST = 192
+CUT5 = 448
+FIRST = 160
 WARM = 3
-ODD_AT, WEIGHTS_AT, PICKED_AT = 56 * 1024, 112 * 1024, 148 * 1024
+ODD_AT, WEIGHTS_AT, CODES_AT, PICKED_AT = 56 * 1024, 112 * 1024, 120 * 1024, 148 * 1024
 
 
 def tile_list_hbag_none_kernel(tc, xT, w, wgt, offs, out):
     nc = tc.nc
     with ExitStack() as ctx:
         keep = ctx.enter_context(tc.tile_pool(name="keep", bufs=1))
-        reuse = ctx.enter_context(tc.tile_pool(name="reuse", bufs=1))
         laid = ctx.enter_context(tc.tile_pool(name="laid", bufs=1))
         psum = ctx.enter_context(tc.psum_pool(name="psum", bufs=1))
 
         offsets = keep.tile([P, E // LIST], U16, name="offsets")
         weights = laid.tile([P, E], F32, name="weights", offset=WEIGHTS_AT, align_bytes=256)
+        weights_first = laid.tile([P, FIRST], F32, name="weights_first", offset=CODES_AT, align_bytes=256)
         plane = [
             [
                 laid.tile([P, T], F32, name=f"plane{a}_{i}", offset=(i % 2) * ODD_AT + (2 * a + i // 2) * 4 * T, align_bytes=256)
@@ -44,19 +45,26 @@ def tile_list_hbag_none_kernel(tc, xT, w, wgt, offs, out):
         ]
         picked0 = laid.tile([P, PACK, E], F32, name="picked0", offset=PICKED_AT, align_bytes=256)
         picked1 = laid.tile([P, 2, E], F32, name="picked1", offset=PICKED_AT + 16384, align_bytes=256)
-        late = laid.tile([P, 2 * (EARLY + FIRST) + E - FIRST], F32, name="late", offset=PICKED_AT + 24576, align_bytes=256)
+        late = laid.tile([P, 4 * EARLY + C[1]], F32, name="late", offset=PICKED_AT + 24576, align_bytes=256)
         w_raw = [
-            reuse.tile([P, PACK, M], F32, name="w_raw0", offset=0, align_bytes=256),
-            keep.tile([P, PACK, M], F32, name="w_raw1", align_bytes=256),
+            keep.tile([P, PACK, M], F32, name="w_raw0", align_bytes=256),
+            laid.tile([P, PACK, M], F32, name="w_raw1", offset=CODES_AT + 4096, align_bytes=256),
         ]
-        w_bf = [keep.tile([P, M, PACK], BF16, name=f"w_bf{a}", align_bytes=256) for a in range(2)]
+        w_bf = [
+            keep.tile([P, M, PACK], BF16, name="w_bf0", align_bytes=256),
+            laid.tile([P, M, PACK], BF16, name="w_bf1", offset=CODES_AT + 8192, align_bytes=256),
+        ]
         w_codes = [keep.tile([P, M], U32, name=f"w_codes{a}", align_bytes=256) for a in range(2)]
         w_scales = [keep.tile([P, M], U8, name=f"w_scales{a}", align_bytes=256) for a in range(2)]
-        x_bf0 = keep.tile([P, PAIRED, PACK], BF16, name="x_bf0", align_bytes=256)
-        x_codes = [None, keep.tile([P, E], U32, name="x_codes1", align_bytes=256)]
+        x_bf = [keep.tile([P, E, PACK], BF16, name=f"x_bf{a}", align_bytes=256) for a in range(2)]
+        x_codes = [
+            laid.tile([P, E], U32, name="x_codes0", offset=CODES_AT, align_bytes=256),
+            laid.tile([P, E], U32, name="x_codes1", offset=CODES_AT + 4096, align_bytes=256),
+        ]
+        last_codes = laid.tile([P, G, C[1]], U32, name="last_codes", offset=CODES_AT + 8192, align_bytes=256)
         x_scales = [keep.tile([P, E], U8, name=f"x_scales{a}", align_bytes=256) for a in range(2)]
-        acc = [[psum.tile([P, n], F32, name=f"acc{j0}_{m}") for m in range(2)] for j0, n in CHUNKS]
-        staged = [keep.tile([P, S], F32, name=f"staged{m}", align_bytes=256) for m in range(2)]
+        acc = {q: [psum.tile([P, q[1]], F32, name=f"acc{q[0]}_{m}") for m in range(2)] for q in (A, B, C)}
+        staged = {q: keep.tile([P, 2, q[1]], F32, name=f"staged{q[0]}", align_bytes=256) for q in (A, B, C)}
 
         w_rows32 = keep.tile([P, 2, 32], F32, name="wgt_rows", align_bytes=256)
         w_cols32 = keep.tile([P, 2, 32], F32, name="wgt_cols", align_bytes=256)
@@ -67,83 +75,69 @@ def tile_list_hbag_none_kernel(tc, xT, w, wgt, offs, out):
 
         act, dve = nc.scalar.copy, nc.vector.tensor_copy
 
-        def load_plane(a, i):
-            nc.sync.dma_start(out=plane[a][i][:], in_=x_rows[a, i])
-
-        def load_w(a):
+        def load_pass(a, first):
+            for i in range(first, PACK):
+                nc.sync.dma_start(out=plane[a][i][:], in_=x_rows[a, i])
             nc.sync.dma_start(out=w_raw[a][:], in_=w_rows[a])
 
-        def gather(dst, a, i, e0, n):
+        def gather(dst, a, i, e0, n, factors=weights):
             nc.vector.tensor_tensor(
                 dst,
                 plane[a][i][:].indirect(offsets[:, e0 // LIST : (e0 + n) // LIST]),
-                weights[:, e0 : e0 + n],
+                factors[:, e0 : e0 + n],
                 MULT,
             )
 
         def slot(i, e0):
-            two = e0 if e0 < EARLY else e0 - FIRST
             if i == 2:
-                return two
-            return two + (FIRST if EARLY - FIRST <= e0 < EARLY else EARLY + FIRST)
+                return e0 % EARLY
+            if e0 == C[0]:
+                return EARLY + FIRST
+            return EARLY + e0 + (S if e0 < FIRST else 0)
 
-        def gather_late(i, e0, n):
-            gather(late[:, slot(i, e0) : slot(i, e0) + n], 1, i, e0, n)
+        def gather_late(i, e0, n, factors=weights):
+            gather(late[:, slot(i, e0) : slot(i, e0) + n], 1, i, e0, n, factors)
 
-        def pairs0(h, e0, n):
-            act(x_bf0[:, e0 : e0 + n, 2 * h : 2 * h + 2], picked0[:, 2 * h : 2 * h + 2, e0 : e0 + n].rearrange("p t j -> p j t"))
+        def pairs(a, lane, src, e0, n):
+            act(x_bf[a][:, e0 : e0 + n, lane : lane + 2], src[:, :, e0 : e0 + n].rearrange("p t j -> p j t"))
 
         def four_lanes(dst, src):
             act(dst.rearrange("p (u e) t -> p u t e", e=4), src.rearrange("p t (u e) -> p u t e", e=4))
 
-        def early_pairs(c):
-            act(x_bf1[c][:, :, 0:2], picked1[:, :, c * S : (c + 1) * S].rearrange("p t j -> p j t"))
-
         def late_pairs(e0, n):
-            c, j0 = divmod(e0, S)
             lane2, lane3 = slot(2, e0), slot(3, e0)
             step = lane3 - lane2
-            act(x_bf1[c][:, j0 : j0 + n, 2:4], late[:, lane2 : lane2 + 2 * step].rearrange("p (t j) -> p j t", t=2)[:, 0:n, :])
+            act(x_bf[1][:, e0 : e0 + n, 2:4], late[:, lane2 : lane2 + 2 * step].rearrange("p (t j) -> p j t", t=2)[:, 0:n, :])
 
         def quantize(codes, scales, values):
             nc.vector.quantize_mx(out=codes.bitcast(FP8X4), scales=scales, in_=values.rearrange("p j t -> p (j t)"))
 
-        def quantize1(e0, n):
-            c, j0 = divmod(e0, S)
-            quantize(x_codes[1][:, e0 : e0 + n], x_scales[1][:, e0 : e0 + n], x_bf1[c][:, j0 : j0 + n, :])
+        def quantize_w(a):
+            four_lanes(w_bf[a][:], w_raw[a][:])
+            quantize(w_codes[a][:], w_scales[a][:], w_bf[a][:])
 
-        def multiply(a, c, q, start, stop):
-            j0, n = CHUNKS[q]
-            col = c * S + j0
+        def product(a, c, q, start=False, stop=False, j0=0, n=None):
+            n = n or q[1]
+            e0 = c * S + q[0] + j0
+            codes = last_codes[:, c, :] if (a, q) == (0, C) else x_codes[a][:, e0 : e0 + n]
+            quantize(codes, x_scales[a][:, e0 : e0 + n], x_bf[a][:, e0 : e0 + n, :])
             for m in range(2):
                 nc.tensor.matmul_mx(
-                    out=acc[q][m][:],
+                    out=acc[q][m][:, j0 : j0 + n],
                     lhsT=w_codes[a][:, m * P : (m + 1) * P].bitcast(FP8X4),
                     lhsT_scale=w_scales[a][:, m * P : (m + 1) * P],
-                    rhs=x_codes[a][:, col : col + n].bitcast(FP8X4),
-                    rhs_scale=x_scales[a][:, col : col + n],
+                    rhs=codes.bitcast(FP8X4),
+                    rhs_scale=x_scales[a][:, e0 : e0 + n],
                     start=start,
                     stop=stop,
                 )
 
-        def leave(copy, q, m):
-            j0, n = CHUNKS[q]
-            copy(staged[m][:, j0 : j0 + n], acc[q][m][:])
-
-        def store(m, j0, n):
-            nc.sync.dma_start(out=out_rows[:, m, j0 : j0 + n], in_=staged[m][:, j0 : j0 + n])
-
         wgt_halves = wgt.rearrange("p (c s) -> (p c) s", c=G)[0 : P * G : LIST + 1]
         nc.sync.dma_start(out=w_rows32[:].rearrange("p u s -> p (u s)"), in_=wgt_halves.rearrange("u (b s) -> u b s", s=64))
-        load_plane(0, 0)
+        nc.sync.dma_start(out=plane[0][0][:], in_=x_rows[0, 0])
         nc.sync.dma_start(offsets[:], offs)
-        for i in range(1, PACK):
-            load_plane(0, i)
-        load_w(1)
-        for i in range(3):
-            load_plane(1, i)
-        load_w(0)
-        load_plane(1, 3)
+        load_pass(0, 1)
+        load_pass(1, 0)
 
         for h in range(2):
             nc.vector.transpose(w_cols32[:, h, :], w_rows32[:, h, :])
@@ -154,33 +148,28 @@ def tile_list_hbag_none_kernel(tc, xT, w, wgt, offs, out):
             )
         for c in range(G):
             nc.vector.transpose(weights[:, c * S : (c + 1) * S], w_spread[c][:].rearrange("p b u h r -> p (b u h r)"))
+        act(weights_first[:], weights[:, 0:FIRST])
 
         for i in range(PACK):
             gather(picked0[:, i, :], 0, i, 0, E)
             if i == 1:
-                pairs0(0, 0, PAIRED)
-        four_lanes(w_bf[1][:], w_raw[1][:])
-        quantize(w_codes[1][:], w_scales[1][:], w_bf[1][:])
-        pairs0(1, 0, PAIRED)
+                pairs(0, 0, picked0[:, 0:2, :], 0, PAIRED)
+        quantize_w(0)
+        pairs(0, 2, picked0[:, 2:4, :], 0, PAIRED)
+        four_lanes(x_bf[0][:, PAIRED:E, :], picked0[:, :, PAIRED:E])
+
         gather(picked1[:, 0, :], 1, 0, 0, E)
-        x_bf0_end = laid.tile([P, E - PAIRED, PACK], BF16, name="x_bf0_end", offset=2 * 4 * T, align_bytes=256)
-        four_lanes(x_bf0_end[:], picked0[:, :, PAIRED:E])
-        for c in range(G):
-            gather(picked1[:, 1, c * S : (c + 1) * S], 1, 1, c * S, S)
-        x_codes[0] = laid.tile([P, E], U32, name="x_codes0", offset=PICKED_AT, align_bytes=256)
-        for e0, e1 in ((0, S), (S, PAIRED)):
-            quantize(x_codes[0][:, e0:e1], x_scales[0][:, e0:e1], x_bf0[:, e0:e1, :])
-        quantize(x_codes[0][:, PAIRED:E], x_scales[0][:, PAIRED:E], x_bf0_end[:])
-        x_bf1 = [keep.tile([P, S, PACK], BF16, name="x_bf1_0", align_bytes=256)]
-        early_pairs(0)
+        for e0, e1 in ((0, CUT5), (CUT5, E)):
+            gather(picked1[:, 1, e0:e1], 1, 1, e0, e1 - e0)
+            pairs(1, 0, picked1[:], e0, e1 - e0)
         gather_late(2, 0, EARLY)
-        four_lanes(w_bf[0][:], w_raw[0][:])
-        x_bf1.append(reuse.tile([P, S, PACK], BF16, name="x_bf1_1", offset=0, align_bytes=256))
-        early_pairs(1)
-        quantize(w_codes[0][:], w_scales[0][:], w_bf[0][:])
+
+        gather_late(3, 0, FIRST, weights_first)
+        late_pairs(0, FIRST)
+        gather_late(3, FIRST, C[0] - FIRST)
+        late_pairs(FIRST, C[0] - FIRST)
         for c in range(G):
-            for q in range(len(CHUNKS)):
-                multiply(0, c, q, c == 0, False)
+            product(0, c, A, start=c == 0)
         unread = psum.tile([P, WARM, P], F32, name="unread")
         for u in range(WARM):
             nc.tensor.matmul_mx(
@@ -192,34 +181,31 @@ def tile_list_hbag_none_kernel(tc, xT, w, wgt, offs, out):
                 start=True,
                 stop=True,
             )
-
-        head = EARLY - FIRST
-        gather_late(3, head, FIRST)
-        late_pairs(head, FIRST)
-        gather_late(3, 0, 256)
-        late_pairs(0, 256)
-        gather_late(3, 256, head - 256)
-        late_pairs(S, head - S)
-        late_pairs(256, 256)
-        gather_late(3, EARLY, E - EARLY)
-        for e0 in (EARLY, EARLY + 128):
-            gather_late(2, e0, 128)
-            late_pairs(e0, 128)
+        gather_late(3, S, S)
         for c in range(G):
-            quantize1(c * S, 256)
-            multiply(1, c, 0, False, c == 1)
-        quantize1(256, 256)
-        for q in (1, 2):
-            multiply(1, 0, q, False, False)
-        for q in (1, 2):
-            quantize1(S + CHUNKS[q][0], 128)
-            multiply(1, 1, q, False, True)
-        half = S // 2
+            product(0, c, B, start=c == 0)
+        gather_late(2, EARLY, E - EARLY)
+        quantize_w(1)
+        for j0 in (0, P):
+            late_pairs(S + j0, P)
+        late_pairs(S + B[0], B[1])
+        late_pairs(S + C[0], C[1])
+        product(1, 0, A)
+        gather_late(3, C[0], C[1])
+        late_pairs(C[0], C[1])
+        for j0 in (0, P):
+            product(1, 1, A, stop=j0 == P, j0=j0, n=P)
+        for c in range(G):
+            product(1, c, B, stop=c == 1)
+        for c in range(G):
+            product(0, c, C, start=c == 0)
+        product(1, 1, C)
+        product(1, 0, C, stop=True)
+
         for m in range(2):
-            leave(act, 0, m)
-            store(m, 0, half)
-        for q in (1, 2):
-            leave(dve, q, 0)
-            leave(act, q, 1)
-        for m in range(2):
-            store(m, half, half)
+            act(staged[A][:, m, :], acc[A][m][:])
+            nc.sync.dma_start(out=out_rows[:, m, 0 : A[1]], in_=staged[A][:, m, :])
+        for q in (B, C):
+            dve(staged[q][:, 0, :], acc[q][0][:])
+            act(staged[q][:, 1, :], acc[q][1][:])
+            nc.sync.dma_start(out=out_rows[:, :, q[0] : q[0] + q[1]], in_=staged[q][:])

@@ -18,6 +18,7 @@ PACK = 4
 LIST = 16
 E = G * S
 A, B, C = (0, 256), (256, 128), (384, 128)
+HELD = [(1, B), (0, C), (1, C)]
 PAIRED = 768
 EARLY = 768
 CUT5 = 448
@@ -61,7 +62,7 @@ def tile_list_hbag_none_kernel(tc, xT, w, wgt, offs, out):
             laid.tile([P, E], U32, name="x_codes0", offset=CODES_AT, align_bytes=256),
             laid.tile([P, E], U32, name="x_codes1", offset=CODES_AT + 4096, align_bytes=256),
         ]
-        last_codes = laid.tile([P, G, C[1]], U32, name="last_codes", offset=CODES_AT + 8192, align_bytes=256)
+        last_codes = laid.tile([P, len(HELD), P], U32, name="last_codes", offset=CODES_AT + 8192, align_bytes=256)
         x_scales = [keep.tile([P, E], U8, name=f"x_scales{a}", align_bytes=256) for a in range(2)]
         acc = {q: [psum.tile([P, q[1]], F32, name=f"acc{q[0]}_{m}") for m in range(2)] for q in (A, B, C)}
         staged = {q: keep.tile([P, 2, q[1]], F32, name=f"staged{q[0]}", align_bytes=256) for q in (A, B, C)}
@@ -92,7 +93,7 @@ def tile_list_hbag_none_kernel(tc, xT, w, wgt, offs, out):
             if i == 2:
                 return e0 % EARLY
             if e0 == C[0]:
-                return EARLY + FIRST
+                return EARLY + S
             return EARLY + e0 + (S if e0 < FIRST else 0)
 
         def gather_late(i, e0, n, factors=weights):
@@ -119,7 +120,7 @@ def tile_list_hbag_none_kernel(tc, xT, w, wgt, offs, out):
         def product(a, c, q, start=False, stop=False, j0=0, n=None):
             n = n or q[1]
             e0 = c * S + q[0] + j0
-            codes = last_codes[:, c, :] if (a, q) == (0, C) else x_codes[a][:, e0 : e0 + n]
+            codes = last_codes[:, HELD.index((c, q)), :] if a == 0 and (c, q) in HELD else x_codes[a][:, e0 : e0 + n]
             quantize(codes, x_scales[a][:, e0 : e0 + n], x_bf[a][:, e0 : e0 + n, :])
             for m in range(2):
                 nc.tensor.matmul_mx(
@@ -182,19 +183,20 @@ def tile_list_hbag_none_kernel(tc, xT, w, wgt, offs, out):
                 stop=True,
             )
         gather_late(3, S, S)
-        for c in range(G):
-            product(0, c, B, start=c == 0)
+        product(0, 0, B, start=True)
         gather_late(2, EARLY, E - EARLY)
         quantize_w(1)
         for j0 in (0, P):
             late_pairs(S + j0, P)
         late_pairs(S + B[0], B[1])
         late_pairs(S + C[0], C[1])
-        product(1, 0, A)
+        for j0 in (0, P):
+            product(1, 0, A, j0=j0, n=P)
         gather_late(3, C[0], C[1])
         late_pairs(C[0], C[1])
         for j0 in (0, P):
             product(1, 1, A, stop=j0 == P, j0=j0, n=P)
+        product(0, 1, B)
         for c in range(G):
             product(1, c, B, stop=c == 1)
         for c in range(G):

@@ -64,7 +64,8 @@ def tile_list_hbag_none_kernel(tc, xT, w, wgt, offs, out):
         ]
         last_codes = laid.tile([P, len(HELD), P], U32, name="last_codes", offset=CODES_AT + 8192, align_bytes=256)
         x_scales = [keep.tile([P, E], U8, name=f"x_scales{a}", align_bytes=256) for a in range(2)]
-        acc = {q: [psum.tile([P, q[1]], F32, name=f"acc{q[0]}_{m}") for m in range(2)] for q in (A, B, C)}
+        acc = {(q, m): psum.tile([P, q[1]], F32, name=f"acc{q[0]}_{m}") for q in (A, B, C) for m in range(2) if (q, m) != (A, 0)}
+        acc_first = [psum.tile([P, P], F32, name=f"acc_first{h}") for h in range(2)]
         staged = {q: keep.tile([P, 2, q[1]], F32, name=f"staged{q[0]}", align_bytes=256) for q in (A, B, C)}
 
         w_rows32 = keep.tile([P, 2, 32], F32, name="wgt_rows", align_bytes=256)
@@ -122,15 +123,19 @@ def tile_list_hbag_none_kernel(tc, xT, w, wgt, offs, out):
             e0 = c * S + q[0] + j0
             codes = last_codes[:, HELD.index((c, q)), :] if a == 0 and (c, q) in HELD else x_codes[a][:, e0 : e0 + n]
             quantize(codes, x_scales[a][:, e0 : e0 + n], x_bf[a][:, e0 : e0 + n, :])
-            for m in range(2):
+            if q == A:
+                parts = [(0, acc_first[j // P][:], j - j0, P, stop or (a, c) == (1, 1)) for j in range(j0, j0 + n, P)]
+            else:
+                parts = [(0, acc[q, 0][:], 0, n, stop)]
+            for m, sums, k0, k, last in parts + [(1, acc[q, 1][:, j0 : j0 + n], 0, n, stop)]:
                 nc.tensor.matmul_mx(
-                    out=acc[q][m][:, j0 : j0 + n],
+                    out=sums,
                     lhsT=w_codes[a][:, m * P : (m + 1) * P].bitcast(FP8X4),
                     lhsT_scale=w_scales[a][:, m * P : (m + 1) * P],
-                    rhs=codes.bitcast(FP8X4),
-                    rhs_scale=x_scales[a][:, e0 : e0 + n],
+                    rhs=codes[:, k0 : k0 + k].bitcast(FP8X4),
+                    rhs_scale=x_scales[a][:, e0 + k0 : e0 + k0 + k],
                     start=start,
-                    stop=stop,
+                    stop=last,
                 )
 
         wgt_halves = wgt.rearrange("p (c s) -> (p c) s", c=G)[0 : P * G : LIST + 1]
@@ -204,10 +209,12 @@ def tile_list_hbag_none_kernel(tc, xT, w, wgt, offs, out):
         product(1, 1, C)
         product(1, 0, C, stop=True)
 
-        for m in range(2):
-            act(staged[A][:, m, :], acc[A][m][:])
-            nc.sync.dma_start(out=out_rows[:, m, 0 : A[1]], in_=staged[A][:, m, :])
+        for h in range(2):
+            act(staged[A][:, 0, h * P : (h + 1) * P], acc_first[h][:])
+        nc.sync.dma_start(out=out_rows[:, 0, 0 : A[1]], in_=staged[A][:, 0, :])
+        act(staged[A][:, 1, :], acc[A, 1][:])
+        nc.sync.dma_start(out=out_rows[:, 1, 0 : A[1]], in_=staged[A][:, 1, :])
         for q in (B, C):
-            dve(staged[q][:, 0, :], acc[q][0][:])
-            act(staged[q][:, 1, :], acc[q][1][:])
+            dve(staged[q][:, 0, :], acc[q, 0][:])
+            act(staged[q][:, 1, :], acc[q, 1][:])
             nc.sync.dma_start(out=out_rows[:, :, q[0] : q[0] + q[1]], in_=staged[q][:])

from contextlib import ExitStack

import concourse.mybir as mybir

G, K, M, T, S = 2, 1024, 256, 2048, 512
FLOPS = 2 * G * K * M * S

F32 = mybir.dt.float32
BF16 = mybir.dt.bfloat16
U32 = mybir.dt.uint32
U16 = mybir.dt.uint16
U8 = mybir.dt.uint8
FP8X4 = mybir.dt.float8_e4m3fn_x4
MULT = mybir.AluOpType.mult

P = 128
PACK = 4
LIST = 16
E = G * S
A, B, C = (0, 256), (256, 128), (384, 128)
HELD = [(1, B), (0, C), (1, C)]
PAIRED = 768
EARLY = 768
CUT5 = 448
FIRST = 160
WARM = 3
ODD_AT, WEIGHTS_AT, CODES_AT, PICKED_AT = 56 * 1024, 112 * 1024, 120 * 1024, 148 * 1024


def tile_list_hbag_none_kernel(tc, xT, w, wgt, offs, out):
    nc = tc.nc
    with ExitStack() as ctx:
        keep = ctx.enter_context(tc.tile_pool(name="keep", bufs=1))
        laid = ctx.enter_context(tc.tile_pool(name="laid", bufs=1))
        psum = ctx.enter_context(tc.psum_pool(name="psum", bufs=1))

        offsets = keep.tile([P, E // LIST], U16, name="offsets")
        weights = laid.tile([P, E], F32, name="weights", offset=WEIGHTS_AT, align_bytes=256)
        weights_first = laid.tile([P, FIRST], F32, name="weights_first", offset=CODES_AT, align_bytes=256)
        plane = [
            [
                laid.tile([P, T], F32, name=f"plane{a}_{i}", offset=(i % 2) * ODD_AT + (2 * a + i // 2) * 4 * T, align_bytes=256)
                for i in range(PACK)
            ]
            for a in range(2)
        ]
        picked0 = laid.tile([P, PACK, E], F32, name="picked0", offset=PICKED_AT, align_bytes=256)
        picked1 = laid.tile([P, 2, E], F32, name="picked1", offset=PICKED_AT + 16384, align_bytes=256)
        late = laid.tile([P, 4 * EARLY + C[1]], F32, name="late", offset=PICKED_AT + 24576, align_bytes=256)
        w_raw = [
            keep.tile([P, PACK, M], F32, name="w_raw0", align_bytes=256),
            laid.tile([P, PACK, M], F32, name="w_raw1", offset=CODES_AT + 4096, align_bytes=256),
        ]
        w_bf = [
            keep.tile([P, M, PACK], BF16, name="w_bf0", align_bytes=256),
            laid.tile([P, M, PACK], BF16, name="w_bf1", offset=CODES_AT + 8192, align_bytes=256),
        ]
        w_codes = [keep.tile([P, M], U32, name=f"w_codes{a}", align_bytes=256) for a in range(2)]
        w_scales = [keep.tile([P, M], U8, name=f"w_scales{a}", align_bytes=256) for a in range(2)]
        x_bf = [keep.tile([P, E, PACK], BF16, name=f"x_bf{a}", align_bytes=256) for a in range(2)]
        x_codes = [
            laid.tile([P, E], U32, name="x_codes0", offset=CODES_AT, align_bytes=256),
            laid.tile([P, E], U32, name="x_codes1", offset=CODES_AT + 4096, align_bytes=256),
        ]
        last_codes = laid.tile([P, len(HELD), P], U32, name="last_codes", offset=CODES_AT + 8192, align_bytes=256)
        x_scales = [keep.tile([P, E], U8, name=f"x_scales{a}", align_bytes=256) for a in range(2)]
        acc = {(q, m): psum.tile([P, q[1]], F32, name=f"acc{q[0]}_{m}") for q in (A, B, C) for m in range(2) if (q, m) != (A, 0)}
        acc_first = [psum.tile([P, P], F32, name=f"acc_first{h}") for h in range(2)]
        staged = {q: keep.tile([P, 2, q[1]], F32, name=f"staged{q[0]}", align_bytes=256) for q in (A, B, C)}

        w_rows32 = keep.tile([P, 2, 32], F32, name="wgt_rows", align_bytes=256)
        w_cols32 = keep.tile([P, 2, 32], F32, name="wgt_cols", align_bytes=256)
        w_spread = [keep.tile([P, 8, 2, 2, 16], F32, name=f"wgt_spread{c}", align_bytes=256) for c in range(G)]
        x_rows = xT.rearrange("(a p i) t -> a i p t", a=2, i=PACK)
        w_rows = w.rearrange("(a p i) n -> a p i n", a=2, i=PACK)
        out_rows = out.rearrange("(m p) j -> p m j", p=P)

        act, dve = nc.scalar.copy, nc.vector.tensor_copy

        def load_pass(a, first):
            for i in range(first, PACK):
                nc.sync.dma_start(out=plane[a][i][:], in_=x_rows[a, i])
            nc.sync.dma_start(out=w_raw[a][:], in_=w_rows[a])

        def gather(dst, a, i, e0, n, factors=weights):
            nc.vector.tensor_tensor(
                dst,
                plane[a][i][:].indirect(offsets[:, e0 // LIST : (e0 + n) // LIST]),
                factors[:, e0 : e0 + n],
                MULT,
            )

        def slot(i, e0):
            if i == 2:
                return e0 % EARLY
            if e0 == C[0]:
                return EARLY + S
            return EARLY + e0 + (S if e0 < FIRST else 0)

        def gather_late(i, e0, n, factors=weights):
            gather(late[:, slot(i, e0) : slot(i, e0) + n], 1, i, e0, n, factors)

        def pairs(a, lane, src, e0, n):
            act(x_bf[a][:, e0 : e0 + n, lane : lane + 2], src[:, :, e0 : e0 + n].rearrange("p t j -> p j t"))

        def four_lanes(dst, src):
            act(dst.rearrange("p (u e) t -> p u t e", e=4), src.rearrange("p t (u e) -> p u t e", e=4))

        def late_pairs(e0, n):
            lane2, lane3 = slot(2, e0), slot(3, e0)
            step = lane3 - lane2
            act(x_bf[1][:, e0 : e0 + n, 2:4], late[:, lane2 : lane2 + 2 * step].rearrange("p (t j) -> p j t", t=2)[:, 0:n, :])

        def quantize(codes, scales, values):
            nc.vector.quantize_mx(out=codes.bitcast(FP8X4), scales=scales, in_=values.rearrange("p j t -> p (j t)"))

        def quantize_w(a):
            four_lanes(w_bf[a][:], w_raw[a][:])
            quantize(w_codes[a][:], w_scales[a][:], w_bf[a][:])

        def product(a, c, q, start=False, stop=False, j0=0, n=None):
            n = n or q[1]
            e0 = c * S + q[0] + j0
            codes = last_codes[:, HELD.index((c, q)), :] if a == 0 and (c, q) in HELD else x_codes[a][:, e0 : e0 + n]
            quantize(codes, x_scales[a][:, e0 : e0 + n], x_bf[a][:, e0 : e0 + n, :])
            if q == A:
                parts = [(0, acc_first[j // P][:], j - j0, P, stop or (a, c) == (1, 1)) for j in range(j0, j0 + n, P)]
            else:
                parts = [(0, acc[q, 0][:], 0, n, stop)]
            for m, sums, k0, k, last in parts + [(1, acc[q, 1][:, j0 : j0 + n], 0, n, stop)]:
                nc.tensor.matmul_mx(
                    out=sums,
                    lhsT=w_codes[a][:, m * P : (m + 1) * P].bitcast(FP8X4),
                    lhsT_scale=w_scales[a][:, m * P : (m + 1) * P],
                    rhs=codes[:, k0 : k0 + k].bitcast(FP8X4),
                    rhs_scale=x_scales[a][:, e0 + k0 : e0 + k0 + k],
                    start=start,
                    stop=last,
                )

        wgt_halves = wgt.rearrange("p (c s) -> (p c) s", c=G)[0 : P * G : LIST + 1]
        nc.sync.dma_start(out=w_rows32[:].rearrange("p u s -> p (u s)"), in_=wgt_halves.rearrange("u (b s) -> u b s", s=64))
        nc.sync.dma_start(out=plane[0][0][:], in_=x_rows[0, 0])
        nc.sync.dma_start(offsets[:], offs)
        load_pass(0, 1)
        load_pass(1, 0)

        for h in range(2):
            nc.vector.transpose(w_cols32[:, h, :], w_rows32[:, h, :])
        for c in range(G):
            dve(
                w_spread[c][:],
                w_cols32[:].rearrange("p u (h b) -> p b u h", h=2)[:, 8 * c : 8 * (c + 1)].unsqueeze(4).to_broadcast([P, 8, 2, 2, 16]),
            )
        for c in range(G):
            nc.vector.transpose(weights[:, c * S : (c + 1) * S], w_spread[c][:].rearrange("p b u h r -> p (b u h r)"))
        act(weights_first[:], weights[:, 0:FIRST])

        for i in range(PACK):
            gather(picked0[:, i, :], 0, i, 0, E)
            if i == 1:
                pairs(0, 0, picked0[:, 0:2, :], 0, PAIRED)
        quantize_w(0)
        pairs(0, 2, picked0[:, 2:4, :], 0, PAIRED)
        four_lanes(x_bf[0][:, PAIRED:E, :], picked0[:, :, PAIRED:E])

        gather(picked1[:, 0, :], 1, 0, 0, E)
        for e0, e1 in ((0, CUT5), (CUT5, E)):
            gather(picked1[:, 1, e0:e1], 1, 1, e0, e1 - e0)
            pairs(1, 0, picked1[:], e0, e1 - e0)
        gather_late(2, 0, EARLY)

        gather_late(3, 0, FIRST, weights_first)
        late_pairs(0, FIRST)
        gather_late(3, FIRST, C[0] - FIRST)
        late_pairs(FIRST, C[0] - FIRST)
        for c in range(G):
            product(0, c, A, start=c == 0)
        unread = psum.tile([P, WARM, P], F32, name="unread")
        for u in range(WARM):
            nc.tensor.matmul_mx(
                out=unread[:, u, :],
                lhsT=w_codes[0][:, 0:P].bitcast(FP8X4),
                lhsT_scale=w_scales[0][:, 0:P],
                rhs=x_codes[0][:, 0:P].bitcast(FP8X4),
                rhs_scale=x_scales[0][:, 0:P],
                start=True,
                stop=True,
            )
        gather_late(3, S, S)
        product(0, 0, B, start=True)
        gather_late(2, EARLY, E - EARLY)
        quantize_w(1)
        for j0 in (0, P):
            late_pairs(S + j0, P)
        late_pairs(S + B[0], B[1])
        late_pairs(S + C[0], C[1])
        for j0 in (0, P):
            product(1, 0, A, j0=j0, n=P)
        gather_late(3, C[0], C[1])
        late_pairs(C[0], C[1])
        for j0 in (0, P):
            product(1, 1, A, stop=j0 == P, j0=j0, n=P)
        product(0, 1, B)
        for c in range(G):
            product(1, c, B, stop=c == 1)
        for c in range(G):
            product(0, c, C, start=c == 0)
        product(1, 1, C)
        product(1, 0, C, stop=True)

        for h in range(2):
            act(staged[A][:, 0, h * P : (h + 1) * P], acc_first[h][:])
        nc.sync.dma_start(out=out_rows[:, 0, 0 : A[1]], in_=staged[A][:, 0, :])
        act(staged[A][:, 1, :], acc[A, 1][:])
        nc.sync.dma_start(out=out_rows[:, 1, 0 : A[1]], in_=staged[A][:, 1, :])
        for q in (B, C):
            dve(staged[q][:, 0, :], acc[q, 0][:])
            act(staged[q][:, 1, :], acc[q, 1][:])
            nc.sync.dma_start(out=out_rows[:, :, q[0] : q[0] + q[1]], in_=staged[q][:])
